import numpy as np, ml_dtypes
CORES = [6,15,38,47]
N = 4
BF = ml_dtypes.bfloat16
def f(rng, *shape):
    return (rng.standard_normal(shape, dtype=np.float32) * np.exp2(rng.integers(-2, 3, shape[:-1] + (1,)))).astype(BF)
def wide(rng, *shape):
    v = f(rng, *shape).astype(np.float32); k = shape[:-2] + (1, shape[-1])
    return (v * np.exp2(rng.integers(-6, 7, k)) * (rng.random(k) > 0.0625)).astype(BF)
def gentries(a):
    return np.ascontiguousarray(a.reshape(8, 16, -1).transpose(0, 2, 1)).reshape(8, -1)
def gtable(e):
    e = np.asarray(e); return np.ascontiguousarray(e.reshape(8, -1, 16).transpose(0, 2, 1)).reshape(128, -1).astype(np.int32)
W, F, U, CAP, SW = 7, 64, 2, 8, 2
C = W * F; Z = C + (W - 1) * N * CAP
def pack(x):
    return np.stack([gtable(v.reshape(8, -1)) for v in x])
def unpack(x):
    return np.stack([gentries(v) for v in x])
def sends(rng, full):
    x = np.argsort(rng.random((N, 8, W - 1, N, F)), axis=-1)[..., :CAP] + F * np.arange(W - 1).reshape(1, 1, W - 1, 1, 1)
    n = rng.integers(0, CAP + 1, (N, 8, W - 1, N, 1)); n[0, :, 0, 1] = CAP
    if full: n[:] = CAP
    keep = (np.argsort(rng.random(x.shape), axis=-1) < n) & (np.arange(N).reshape(N, 1, 1, 1, 1) != np.arange(N).reshape(1, 1, 1, N, 1))
    return np.where(keep, x, Z)
def upwind(rng, far, none):
    s = (N, 8, W, U, F); r = np.arange(N).reshape(N, 1, 1, 1, 1); w = np.arange(W).reshape(1, 1, W, 1, 1)
    v = np.where(rng.random(s) < 0.75, w - 1, (rng.random(s) * w).astype(np.int64))
    near = v * F + rng.integers(0, F, s); away = C + (v * N + (r + 1 + rng.integers(0, N - 1, s)) % N) * CAP + rng.integers(0, CAP, s)
    p = rng.random(s)
    return np.where(w == 0, Z, np.where(p < far, away, np.where(p < far + none, Z, near)))
def draw(rng, o, p, x):
    return {"qs": f(rng, N, 128, C), "rm": (0.5 + 0.5 * rng.random((N, 128, C))).astype(BF), "co": (0.75 * rng.random((N, 128, U * C))).astype(BF),
            "sc": (f(rng, N, 16, 16).astype(np.float32) * np.float32(0.0625)).astype(BF), "seq": pack(o), "up": pack(p), "snd": pack(x)}
def orders(rng):
    return np.argsort(rng.random((N, 8, C)), axis=-1)
def setup_inputs(rng):
    return draw(rng, orders(rng), upwind(rng, 0.5, 0.1), sends(rng, False))
def setup_inputs_full(rng):
    return draw(rng, orders(rng), upwind(rng, 0.9, 0.0), sends(rng, True))
def setup_inputs_chain(rng):
    w = np.arange(W).reshape(1, 1, W, 1, 1); r = np.arange(N).reshape(N, 1, 1, 1, 1); x = sends(rng, True)
    p = np.where(w == 0, Z, C + ((w - 1) * N + (r + 1) % N) * CAP + rng.integers(0, CAP, (N, 8, W, U, F)))
    other = np.arange(N).reshape(N, 1, 1, 1) != np.arange(N).reshape(1, 1, 1, N); a = F * np.arange(W - 1).reshape(1, 1, W - 1, 1)
    x[..., 0] = np.where(other, a, Z); x[..., CAP - 1] = np.where(other, a + F - 1, Z)
    return draw(rng, orders(rng), p, x)
def setup_inputs_alike(rng):
    x = sends(rng, True); x[:] = x[..., :1].copy(); p = upwind(rng, 0.5, 0.1); p = np.repeat(p[:, :, :, :1], U, axis=3)
    o = orders(rng); o[:, 0] = np.arange(C); o[:, 1] = np.arange(C)[::-1]; o[:, 3] = o[:, 2]
    return draw(rng, o, p, x)
def setup_inputs_few(rng):
    x = sends(rng, False); k = int(rng.integers(0, N)); x[k] = Z; x[:, :, :, k] = Z
    d = draw(rng, orders(rng), upwind(rng, 0.08, 0.85), x); d["rm"] = np.where(rng.random(d["rm"].shape) < 0.125, np.float32(0), d["rm"].astype(np.float32)).astype(BF)
    return d
def setup_inputs_spread(rng):
    d = setup_inputs(rng); d["qs"] = wide(rng, N, 128, C); return d
def check_inputs(d):
    bad = []
    if not (np.sort(unpack(d["seq"]), axis=-1) == np.arange(C)).all(): bad.append("seq")
    p = unpack(d["up"]).reshape(N, 8, W, U * F).astype(np.int64); w = np.arange(W).reshape(1, 1, W, 1); r = np.arange(N).reshape(N, 1, 1, 1); s = p - C
    if not ((p == Z) | ((p >= 0) & (p < w * F)) | ((s >= 0) & (s < w * N * CAP) & ((s // CAP) % N != r))).all(): bad.append("up")
    x = unpack(d["snd"]).reshape(N, 8, W - 1, N, CAP).astype(np.int64); w = np.arange(W - 1).reshape(1, 1, W - 1, 1, 1)
    other = np.arange(N).reshape(N, 1, 1, 1, 1) != np.arange(N).reshape(1, 1, 1, N, 1)
    if not ((x == Z) | ((x >= w * F) & (x < w * F + F) & other)).all(): bad.append("snd")
    if not all(np.isfinite(d[k].astype(np.float32)).all() for k in ("qs", "rm", "co", "sc")): bad.append("finite")
    return bad
def reference(qs, rm, co, sc, seq, up, snd):
    o = unpack(seq).astype(np.int64); p = unpack(up).astype(np.int64); x = unpack(snd).astype(np.int64)
    src = qs.astype(np.float64).reshape(N, 8, 16, C); rem = rm.astype(np.float64).reshape(N, 8, 16, C); a = co.astype(np.float64).reshape(N, 8, 16, W, U, F)
    s = sc.astype(np.float64).transpose(0, 2, 1); y = np.zeros((N, 16, C), np.float64)
    for k in range(SW):
        win = np.zeros((N, 8, 16, Z + 1), np.float64)
        for w in range(W):
            c = o[:, :, None, w * F:w * F + F]
            h = np.take_along_axis(win, p[:, :, None, w * U * F:(w + 1) * U * F], 3).reshape(N, 8, 16, U, F)
            v = (np.take_along_axis(src, c, 3) + np.sum(a[:, :, :, w] * h, axis=3)) * np.take_along_axis(rem, c, 3)
            v = np.maximum(v, 0.0)
            win[..., w * F:w * F + F] = v
            if w == W - 1: continue
            for r in range(N):
                for q in range(N):
                    if q == r: continue
                    b = C + (w * N + r) * CAP; e = (w * N + q) * CAP
                    win[q, :, :, b:b + CAP] = np.take_along_axis(win[r], x[r][:, None, e:e + CAP], 2)
        psi = np.zeros((N, 8, 16, C), np.float64); np.put_along_axis(psi, o[:, :, None], win[..., :C], 3)
        flux = np.sum(psi, axis=1); y = y + flux
        src = np.repeat(np.matmul(s, flux)[:, None], 8, axis=1)
    return {"y": y.astype(np.float32)}

@@ -1,0 +1,468 @@
+from concourse.bass import DstId, RemoteDMATransfer
+from concourse.mybir import AluOpType as O, ActivationFunctionType as AF
+
+W, F, U, CAP, SW, NR = 7, 64, 2, 8, 2, 4
+C = W * F
+Z = C + (W - 1) * NR * CAP
+NS = NR * CAP
+BW = F + NS
+HD = 8
+WIN = HD + (W - 1) * BW + F
+BIG = 9.0e29
+DUP = 3
+NX = 5 * 128
+NL = 5 * 64
+CH = 4
+CW = C // CH
+NXS = 110
+
+SCRATCH = {
+    "seq32": ("sbuf", [128, 28], "int32"), "up32": ("sbuf", [128, 56], "int32"), "snd32": ("sbuf", [128, 12], "int32"),
+    "qsb": ("sbuf", [128, C], "bfloat16"), "rmb": ("sbuf", [128, C], "bfloat16"), "cob": ("sbuf", [128, 2 * C], "bfloat16"),
+    "scb": ("sbuf", [128, 16], "bfloat16"), "scf": ("sbuf", [128, 16], "float32"),
+    "seq16": ("sbuf", [128, 28], "uint16"), "snd16": ("sbuf", [128, 12], "uint16"), "up16": ("sbuf", [128, 56], "uint16"),
+    "lst2": ("sbuf", [128, 12], "uint16"), "idx16": ("sbuf", [128, 20], "uint16"), "ups16": ("sbuf", [128, 20], "uint16"),
+    "rmp": ("sbuf", [128, C], "float32"), "cr": ("sbuf", [128, 2 * C], "float32"), "crs": ("sbuf", [128, NL], "float32"),
+    "base0": ("sbuf", [128, WIN], "float32"), "base1": ("sbuf", [128, WIN], "float32"),
+    "bs0": ("sbuf", [128, 160], "float32"), "bs1": ("sbuf", [128, 160], "float32"),
+    "win0": ("sbuf", [128, WIN], "float32"), "win1": ("sbuf", [128, WIN], "float32"),
+    "psic0": ("sbuf", [128, C], "float32"), "psic1": ("sbuf", [128, C], "float32"), "src": ("sbuf", [128, C], "float32"),
+    "dbl": ("sbuf", [128, 264], "float32"), "dbs": ("sbuf", [128, 136], "float32"),
+    "sco": ("sbuf", [128, 136], "float32"), "scs": ("sbuf", [128, 64], "float32"),
+    "ia": ("sbuf", [128, 56], "int32"), "ib": ("sbuf", [128, 56], "int32"),
+    "ft": ("sbuf", [128, 56], "float32"), "fz": ("sbuf", [128, 56], "float32"), "fa": ("sbuf", [128, 56], "float32"),
+    "fb": ("sbuf", [128, 56], "float32"), "fx": ("sbuf", [128, 56], "float32"), "fy": ("sbuf", [128, 56], "float32"),
+    "fv": ("sbuf", [128, 56], "float32"), "upm": ("sbuf", [128, 56], "float32"),
+    "kk": ("sbuf", [128, 20], "float32"), "kl": ("sbuf", [128, 12], "float32"), "x20": ("sbuf", [128, 20], "float32"),
+    "sa": ("sbuf", [128, 12], "float32"), "saf": ("sbuf", [128, 12], "float32"), "la": ("sbuf", [128, 12], "float32"),
+    "lb": ("sbuf", [128, 12], "float32"), "upd": ("sbuf", [128, 20], "float32"),
+    "iot": ("sbuf", [128, NL], "int32"), "iam": ("sbuf", [128, NL], "int32"), "mskw": ("sbuf", [128, NL], "float32"),
+    "ones": ("sbuf", [128, 128], "float32"), "blk0": ("sbuf", [128, 128], "float32"), "blk": ("sbuf", [128, 128], "float32"),
+    "um": ("sbuf", [128, NX], "float32"), "upf": ("sbuf", [128, NX + 8], "float32"), "upx": ("sbuf", [128, NL], "float32"),
+    "cum": ("sbuf", [128, NL + 16], "float32"), "screp": ("sbuf", [128, 128], "float32"),
+    "yf": ("sbuf", [128, C], "float32"), "yo": ("sbuf", [128, C], "float32"),
+    "ps": ("psum", [128, 2048], "float32"), "pf": ("psum", [128, 2048], "float32"),
+}
+for _s in range(SW):
+    for _w in range(W - 1):
+        SCRATCH["sb%d_%d" % (_s, _w)] = ("sbuf", [128, NS], "float32")
+SEMAPHORES = (["x%d" % i for i in range(NXS)] + ["arr%d_%d" % (s, w) for s in range(SW) for w in range(W - 1)]
+              + ["q_v", "q_s", "q_t", "q_g", "sent"])
+PSUM = ("ps", "pf")
+
+
+def send_calls(topo, src, dests):
+    far = [d for d in dests if not topo.mates(topo.chip(src), topo.chip(d))]
+    near = [d for d in dests if topo.mates(topo.chip(src), topo.chip(d))]
+    far.sort(key=lambda d: topo.same_plane(topo.chip(src), topo.chip(d)))
+    calls = []
+    if len(far) == 2 and len(near) == 1:
+        e = [topo.engines(src, d) for d in far]
+        h = len(e[0]) // 2
+        calls.append([(far[0], e[0][:h]), (far[1], e[1][h:])])
+        calls.append([(near[0], topo.engines(src, near[0]))])
+    else:
+        for d in far + near:
+            calls.append([(d, topo.engines(src, d))])
+    return calls
+
+
+def engines_to(topo, src, dst, dests):
+    return sum(len(e) for call in send_calls(topo, src, dests) for d, e in call if d == dst)
+
+
+def rank_program(g, core, T, topo):
+    rank = T.rank_of(core)
+    if rank is None:
+        return
+    cores = list(T.cores)
+    others = [c for c in cores if c != core]
+    queues = {"v": g.vector, "s": g.scalar, "t": g.tensor, "g": g, "y": g.sync}
+    ops = []
+
+    def reg(name, a, b):
+        if name in PSUM:
+            return (name, a // 512 * 512, (b + 511) // 512 * 512)
+        return (name, a, b)
+
+    def R(name, a, b, step=1, p=128):
+        t = T[name]
+        ap = t[0:p, a:b] if step == 1 else t[0:p, a:b:step]
+        return (ap, [reg(name, a, b)])
+
+    def X(name, b, off, oa, ob, a=0):
+        return (T[name][:, a:b].indirect(T[off][:, oa:ob]), [reg(name, a, b), reg(off, oa, ob)])
+
+    def add_op(q, fn, reads, writes, kind="c", n=1, sem=None):
+        rd, wr = [], []
+        for x in reads:
+            rd += x
+        for x in writes:
+            wr += x
+        ops.append({"q": q, "fn": fn, "r": rd, "w": wr, "kind": kind, "n": n, "sem": sem})
+
+    def split(out):
+        return [out[1][0:1]], [out[1][1:]]
+
+    def tt(out, a, b, op):
+        w, r = split(out)
+        add_op("v", lambda: g.vector.tensor_tensor(out=out[0], in0=a[0], in1=b[0], op=op), [a[1], b[1]] + r, w)
+
+    def ts(out, a, s1, op0, s2=None, op1=None):
+        if op1 is None:
+            add_op("v", lambda: g.vector.tensor_scalar(out=out[0], in0=a[0], scalar1=s1, scalar2=None, op0=op0), [a[1]], [out[1]])
+        else:
+            add_op("v", lambda: g.vector.tensor_scalar(out=out[0], in0=a[0], scalar1=s1, scalar2=s2, op0=op0, op1=op1), [a[1]], [out[1]])
+
+    def cp(out, a):
+        w, r = split(out)
+        add_op("v", lambda: g.vector.tensor_copy(out=out[0], in_=a[0]), [a[1]] + r, w)
+
+    def fill(out, v):
+        add_op("v", lambda: g.vector.memset(out[0], v), [], [out[1]])
+
+    def scan(out, d0, d1, op0, op1):
+        add_op("v", lambda: g.vector.tensor_tensor_scan(out=out[0], data0=d0[0], data1=d1[0], initial=0.0, op0=op0, op1=op1),
+               [d0[1], d1[1]], [out[1]])
+
+    def act(out, a, scale=None):
+        if scale is None:
+            add_op("s", lambda: g.scalar.activation(out=out[0], in_=a[0], func=AF.Identity), [a[1]], [out[1]])
+        else:
+            add_op("s", lambda: g.scalar.activation(out=out[0], in_=a[0], func=AF.Identity, scale=scale[0]), [a[1], scale[1]], [out[1]])
+
+    def mm(out, lhsT, rhs):
+        add_op("t", lambda: g.tensor.matmul(out=out[0], lhsT=lhsT[0], rhs=rhs[0], start=True, stop=True), [lhsT[1], rhs[1]], [out[1]])
+
+    def load(q, name, src, p=128):
+        n = SCRATCH[name][1][1]
+        o = R(name, 0, n, 1, p)
+        add_op(q, lambda: queues[q].dma_start(o[0], src[:, :]), [], [o[1]], "dma", 16)
+
+    def iota(out, pattern, base, cm, flag):
+        if flag:
+            add_op("g", lambda: g.iota(out[0], pattern, base, cm, allow_small_or_imprecise_dtypes=True), [], [out[1]])
+        else:
+            add_op("g", lambda: g.iota(out[0], pattern, base, cm), [], [out[1]])
+
+    def keep_if(out, a, pattern, base, cm):
+        add_op("g", lambda: g.affine_select(out[0], a[0], pattern, O.is_ge, 0.0, base, cm), [a[1]], [out[1]])
+
+    def slots(w, q):
+        return HD + BW * w + F + CAP * q
+
+    def send(s, w):
+        sb, win, arr = "sb%d_%d" % (s, w), "win%d" % s, T.sem["arr%d_%d" % (s, w)]
+        a = slots(w, rank)
+
+        def one(call):
+            if len(call) == 1:
+                d, e = call[0]
+                rid, pid = topo.addr(d)[:2]
+                k = T.rank_of(d)
+                return g.remote_dma(out_ap=T[win][:, a:a + CAP], in_ap=T[sb][:, CAP * k:CAP * k + CAP], remote_sem=arr,
+                                    local_sem=T.sem["sent"], pid=pid, routing_id=rid, dma_engine_mask=sum(1 << x for x in e))
+            tr = []
+            for d, e in call:
+                rid, pid = topo.addr(d)[:2]
+                k = T.rank_of(d)
+                tr.append(RemoteDMATransfer(dst_ids=[DstId(rid=rid, pnc=pid)], dma_engine_mask=sum(1 << x for x in e),
+                                            remote_sem=arr, src=T[sb][:, CAP * k:CAP * k + CAP], dst=T[win][:, a:a + CAP]))
+            return g.remote_dma_fused(tr, local_sem=T.sem["sent"])
+
+        for call in send_calls(topo, core, others):
+            add_op("g", lambda call=call: one(call), [[(sb, 0, NS)]], [], "remote", sum(len(e) for d, e in call))
+
+    def arrival(s, w):
+        n = sum(engines_to(topo, c, core, [d for d in cores if d != c]) for c in others)
+        wr = [("win%d" % s, slots(w, T.rank_of(c)), slots(w, T.rank_of(c)) + CAP) for c in others]
+        add_op("ext", None, [], [wr], "ext", n, "arr%d_%d" % (s, w))
+
+    def own(s, w):
+        return R("win%d" % s, HD + BW * w, HD + BW * w + F)
+
+    def chain(s, w):
+        tt(R("dbl", 1, 257, 2), X("win%d" % s, HD + BW * w, "up16", 8 * w, 8 * w + 8), R("cr", 128 * w, 128 * w + 128), O.mult)
+        scan(R("sco", 0, 128), R("dbl", 0, 128), R("dbl", 129, 257), O.add, O.max)
+
+    def finish(s, w):
+        tt(own(s, w), R("sco", 1, 128, 2), R("base%d" % s, F * w, F * w + F), O.add)
+
+    def to_cells(s, w):
+        cp(X("psic%d" % s, C, "seq16", 4 * w, 4 * w + 4), own(s, w))
+
+    def send_first(s, w):
+        tt(R("dbs", 1, 129, 2), X("win%d" % s, HD + BW * w, "ups16", 4 * (w - 1), 4 * w), R("crs", 64 * (w - 1), 64 * w), O.mult)
+        scan(R("scs", 0, 64), R("dbs", 0, 64), R("dbs", 65, 129), O.add, O.max)
+        tt(R("sb%d_%d" % (s, w), 0, NS), R("scs", 1, 64, 2), R("bs%d" % s, NS * (w - 1), NS * w), O.add)
+        send(s, w)
+
+    def prep(s, w):
+        ts(R("dbl", 130, 258, 2), R("base%d" % s, F * w, F * w + F), -1.0, O.mult)
+
+    def prep_first(s, w):
+        ts(R("dbs", 66, 130, 2), R("bs%d" % s, NS * (w - 1), NS * w), -1.0, O.mult)
+
+    def coef(w):
+        for u in range(U):
+            a = 128 * w + 64 * u
+            tt(R("cr", a, a + F), R("cob", a, a + F), R("rmp", F * w, F * w + F), O.mult)
+
+    def send_base(s, a, b):
+        cp(R("bs%d" % s, NS * (a - 1), NS * (b - 1)), X("base%d" % s, WIN, "snd16", 2 * a, 2 * b))
+
+    def self_slots(s):
+        for w in range(W - 1):
+            fill(R("win%d" % s, slots(w, rank), slots(w, rank) + CAP), 0.0)
+
+    load("y", "seq32", T.seq)
+    load("s", "rmb", T.rm)
+    load("y", "qsb", T.qs)
+    load("s", "snd32", T.snd)
+    load("y", "up32", T.up)
+    load("s", "cob", T.co)
+    load("y", "scb", T.sc, 16)
+    iota(R("iot", 0, NL), [[1, NL]], 1024, -1, False)
+    fill(R("ones", 0, 128), 1.0)
+    fill(R("base0", 0, WIN), 0.0)
+    fill(R("dbl", 0, 264), -BIG)
+    fill(R("dbs", 0, 136), -BIG)
+    fill(R("win0", 0, HD), 0.0)
+    iota(R("kl", 0, 12), [[-128, 6], [0, 2]], 0, 0, True)
+    iota(R("kk", 0, 20), [[64, 5], [64, 2], [0, 2]], -64, 0, True)
+    keep_if(R("blk0", 0, 128), R("ones", 0, 128), [[-16, 8], [0, 16]], 0, 1)
+    keep_if(R("blk", 0, 128), R("blk0", 0, 128), [[16, 8], [0, 16]], 15, -1)
+    ts(R("iam", 0, NL), R("iot", 0, NL), 15, O.bitwise_and)
+    ts(R("mskw", 0, NL), R("iam", 0, NL), 0.0, O.is_equal)
+
+    cp(R("seq16", 0, 28), R("seq32", 0, 28))
+    cp(R("rmp", 0, F), X("rmb", C, "seq16", 0, 4))
+    cp(R("snd16", 0, 12), R("snd32", 0, 12))
+    tt(R("base0", 0, F), X("qsb", C, "seq16", 0, 4), R("rmp", 0, F), O.mult)
+    ts(R("sb0_0", 0, NS), X("base0", WIN, "snd16", 0, 2), 0.0, O.max)
+    send(0, 0)
+    act(R("rmp", F, C), X("rmb", C, "seq16", 4, 28))
+    ts(R("ia", 0, 56), R("up32", 0, 56), 0x3C0, O.bitwise_and)
+    ts(R("ib", 0, 56), R("up32", 0, 56), 0x3E0, O.bitwise_and)
+    ts(R("ft", 0, 56), R("up32", 0, 56), float(C), O.is_ge, -4096.0, O.mult)
+    ts(R("fz", 0, 56), R("up32", 0, 56), float(Z), O.is_ge, -648.0, O.mult)
+    ts(R("fa", 0, 56), R("ia", 0, 56), 0.5, O.mult, 8.0, O.add)
+    ts(R("fb", 0, 56), R("ib", 0, 56), 2.0, O.mult, -1272.0, O.add)
+    tt(R("fv", 0, 56), R("up32", 0, 56), R("fz", 0, 56), O.add)
+    tt(R("fx", 0, 56), R("fa", 0, 56), R("ft", 0, 56), O.add)
+    tt(R("fy", 0, 56), R("fx", 0, 56), R("fb", 0, 56), O.max)
+    tt(R("upm", 0, 56), R("fy", 0, 56), R("fv", 0, 56), O.add)
+    cp(R("up16", 0, 56), R("upm", 0, 56))
+    ts(own(0, 0), R("base0", 0, F), 0.0, O.max)
+    tt(R("base0", F, 2 * F), X("qsb", C, "seq16", 4, 8), R("rmp", F, 2 * F), O.mult)
+    prep(0, 1)
+    coef(1)
+    ts(R("la", 0, 12), R("snd32", 0, 12), 2.0, O.mult, 1.0, O.add)
+    tt(R("lb", 0, 12), R("la", 0, 12), R("kl", 0, 12), O.add)
+    ts(R("lst2", 0, 12), R("lb", 0, 12), 128.0, O.min)
+    fill(R("sco", 128, 136), 0.0)
+    self_slots(0)
+    send_base(0, 1, 2)
+    for i in range(16):
+        act(R("um", i, NX, 16), R("upm", 8, 48), R("mskw", i, i + 1))
+    mm(R("ps", 0, 320), R("blk", 0, 128), R("um", 0, 320))
+    mm(R("ps", 512, 832), R("blk", 0, 128), R("um", 320, 640))
+    act(R("upf", 0, 320), R("ps", 0, 320))
+    act(R("upf", 320, 640), R("ps", 512, 832))
+    arrival(0, 0)
+
+    for w in range(1, W):
+        last = w == W - 1
+        if w < DUP:
+            chain(0, w)
+            tt(R("sb0_%d" % w, 0, NS), X("sco", 136, "lst2", 2 * w, 2 * w + 2), R("bs0", NS * (w - 1), NS * w), O.add)
+            send(0, w)
+            finish(0, w)
+        elif not last:
+            send_first(0, w)
+            chain(0, w)
+            finish(0, w)
+        else:
+            chain(0, w)
+            tt(X("psic0", C, "seq16", 4 * w, 4 * w + 4), R("sco", 1, 128, 2), R("base0", F * w, F * w + F), O.add)
+        if w == 1:
+            tt(R("base0", 2 * F, C), X("qsb", C, "seq16", 8, 28), R("rmp", 2 * F, C), O.mult)
+            prep(0, 2)
+            coef(2)
+            send_base(0, 2, 6)
+            fill(R("upf", NX, NX + 8), 0.0)
+            fill(R("cum", 0, 16), 0.0)
+            fill(R("cr", 128 + NX, 128 + NX + 8), 0.0)
+            ts(R("sa", 0, 12), R("snd32", 0, 12), float(Z), O.is_ge, 512.0, O.mult)
+            tt(R("saf", 0, 12), R("snd32", 0, 12), R("sa", 0, 12), O.add)
+            for u in range(U):
+                for c in range(2):
+                    tt(R("x20", 2 * u + c, 20, 4), R("saf", 2 + c, 12, 2), R("kk", 2 * u + c, 20, 4), O.add)
+            ts(R("idx16", 0, 20), R("x20", 0, 20), float(NX), O.min)
+            for x in range(3, W - 1):
+                coef(x)
+        if w == 2:
+            prep(0, 3)
+            tt(R("upx", 0, NL), X("upf", NX + 8, "idx16", 0, 20), R("mskw", 0, NL), O.mult)
+            scan(R("cum", 16, NL + 16), R("upx", 0, NL), R("upx", 0, NL), O.add, O.max)
+            tt(R("upd", 0, 20), R("cum", 31, NL + 16, 16), R("cum", 15, NL, 16), O.subtract)
+            cp(R("ups16", 0, 20), R("upd", 0, 20))
+            cp(R("crs", 0, NL), X("cr", 128 + NX + 8, "idx16", 0, 20, 128))
+            prep_first(0, 3)
+        if w == 3:
+            coef(6)
+        if 3 <= w < W - 1:
+            prep(0, w + 1)
+            if w + 1 < W - 1:
+                prep_first(0, w + 1)
+        if w == 3:
+            for x in range(3):
+                to_cells(0, x)
+        if 3 <= w < W - 1:
+            to_cells(0, w)
+        if w == 4:
+            fill(R("base1", 0, WIN), 0.0)
+            fill(R("win1", 0, HD), 0.0)
+            cp(R("scf", 0, 16, 1, 16), R("scb", 0, 16, 1, 16))
+            mm(R("pf", 0, 16), R("mskw", 0, 128, 1, 16), R("scf", 0, 16, 1, 16))
+            for i in range(8):
+                act(R("screp", 16 * i, 16 * i + 16), R("pf", 0, 16))
+        if w == 5:
+            self_slots(1)
+        if not last:
+            arrival(0, w)
+
+    for i in range(CH):
+        mm(R("ps", 512 * i, 512 * i + CW), R("screp", 0, 128), R("psic0", CW * i, CW * i + CW))
+    for i in range(CH):
+        o, a = R("src", CW * i, CW * i + CW), R("ps", 512 * i, 512 * i + CW)
+        if i % 2 == 0:
+            act(o, a)
+        else:
+            cp(o, a)
+    tt(R("base1", 0, F), X("src", C, "seq16", 0, 4), R("rmp", 0, F), O.mult)
+    ts(R("sb1_0", 0, NS), X("base1", WIN, "snd16", 0, 2), 0.0, O.max)
+    send(1, 0)
+    for i in range(CH):
+        mm(R("pf", 512 * i, 512 * i + CW, 1, 16), R("mskw", 0, 16), R("psic0", CW * i, CW * i + CW))
+    for i in range(CH):
+        act(R("yf", CW * i, CW * i + CW, 1, 16), R("pf", 512 * i, 512 * i + CW, 1, 16))
+    ts(own(1, 0), R("base1", 0, F), 0.0, O.max)
+    tt(R("base1", F, C), X("src", C, "seq16", 4, 28), R("rmp", F, C), O.mult)
+    send_base(1, 1, 6)
+    prep_first(1, 1)
+    prep(1, 1)
+    to_cells(1, 0)
+    arrival(1, 0)
+
+    for w in range(1, W):
+        if w < W - 1:
+            send_first(1, w)
+            chain(1, w)
+            finish(1, w)
+            prep(1, w + 1)
+            if w + 1 < W - 1:
+                prep_first(1, w + 1)
+            to_cells(1, w)
+            arrival(1, w)
+        else:
+            chain(1, w)
+            tt(X("psic1", C, "seq16", 4 * w, 4 * w + 4), R("sco", 1, 128, 2), R("base1", F * w, F * w + F), O.add)
+
+    for i in range(CH):
+        mm(R("pf", 512 * i, 512 * i + CW, 1, 16), R("mskw", 0, 16), R("psic1", CW * i, CW * i + CW))
+    for i in range(CH):
+        a, b = CW * i, CW * i + CW
+        tt(R("yo", a, b, 1, 16), R("pf", 512 * i, 512 * i + CW, 1, 16), R("yf", a, b, 1, 16), O.add)
+        q = "y" if i % 2 == 1 else "s"
+        add_op(q, lambda q=q, a=a, b=b: queues[q].dma_start(T.y[:, a:b], T.yo[0:16, a:b]), [[("yo", a, b)]], [[("y", a, b)]], "dma", 16)
+
+    emit(g, T, queues, ops)
+
+
+def clash(a, b):
+    for x in a["w"]:
+        for y in b["r"] + b["w"]:
+            if x[0] == y[0] and x[1] < y[2] and y[1] < x[2]:
+                return True
+    for x in a["r"]:
+        for y in b["w"] + (b["r"] if x[0] in PSUM and a["q"] != b["q"] else []):
+            if x[0] == y[0] and x[1] < y[2] and y[1] < x[2]:
+                return True
+    return False
+
+
+def plan_waits(ops, flagged):
+    known, issued, start, waits, new = {}, {}, {}, [], set(flagged)
+    for i, o in enumerate(ops):
+        ws = []
+        q = o["q"]
+        if o["kind"] == "ext":
+            start[i] = 0
+            waits.append(ws)
+            continue
+        k = known.get(q, 0)
+        mine = issued.setdefault(q, [])
+        for j in range(i - 1, -1, -1):
+            if k >> j & 1 or not clash(o, ops[j]):
+                continue
+            p = ops[j]
+            if p["kind"] == "remote":
+                raise ValueError("a call waits for a message's source")
+            if p["q"] == q and p["kind"] == "c" and j not in flagged:
+                ws.append(("q", len(mine)))
+                for m in mine:
+                    k |= 1 << m | start[m]
+            else:
+                ws.append(("u", j))
+                k |= 1 << j | start[j]
+                if p["kind"] == "c":
+                    new.add(j)
+        start[i] = k
+        known[q] = k
+        if o["kind"] == "c" and i not in flagged:
+            mine.append(i)
+        waits.append(ws)
+    return waits, new
+
+
+def emit(g, T, queues, ops):
+    flagged = set()
+    while True:
+        waits, new = plan_waits(ops, flagged)
+        if new == flagged:
+            break
+        flagged = new
+    names = {}
+    for i, o in enumerate(ops):
+        if o["kind"] == "ext":
+            names[i] = o["sem"]
+        elif o["kind"] == "dma" or i in flagged:
+            names[i] = "x%d" % len([k for k in names if names[k][0] == "x"])
+    count, done, sent, waited = {}, {}, 0, set()
+    for i, o in enumerate(ops):
+        if o["kind"] == "ext":
+            continue
+        q = o["q"]
+        for kind, v in waits[i]:
+            if kind == "q":
+                queues[q].wait_ge(T.sem["q_" + q], v)
+                done[q] = v
+            else:
+                queues[q].wait_ge(T.sem[names[v]], ops[v]["n"])
+                waited.add(v)
+        x = o["fn"]()
+        if o["kind"] == "remote":
+            sent += o["n"]
+        elif i in names:
+            x.then_inc(T.sem[names[i]], o["n"])
+        else:
+            x.then_inc(T.sem["q_" + q], 1)
+            count[q] = count.get(q, 0) + 1
+    for q in count:
+        if done.get(q, 0) < count[q]:
+            queues[q].wait_ge(T.sem["q_" + q], count[q])
+    g.wait_ge(T.sem["sent"], sent)
+    for i, o in enumerate(ops):
+        if i in names and i not in waited:
+            queues[o["q"]].wait_ge(T.sem[names[i]], o["n"])

@@ -5,49 +5,75 @@ W, F, U, CAP, SW, NR = 7, 64, 2, 8, 2, 4
 C = W * F
 Z = C + (W - 1) * NR * CAP
 NS = NR * CAP
-BW = F + NS
-HD = 8
-WIN = HD + (W - 1) * BW + F
+BW = 328
+HD = 104
+WIN = HD + BW * (W - 1) + 192
+CR = 136
 BIG = 9.0e29
-DUP = 3
-NX = 5 * 128
-NL = 5 * 64
-CH = 4
-CW = C // CH
-NXS = 110
+OFF = 4096.0
+CELLS = (128, 128, 96, 96)
+KQ = {"v": 8, "s": 8, "t": 2, "g": 2}
+NXS = 108
+FULL = {(0, 2), (0, 4), (1, 0), (1, 2), (1, 4)}
+PLAIN = {(0, 0): CAP, (0, 1): 3 * CAP}
+PAIRS = (3, 5, 1)
+
+
+def own_at(w):
+    return HD + BW * w
+
+
+def slot_at(w):
+    return HD + BW * w + 200
+
 
 SCRATCH = {
     "seq32": ("sbuf", [128, 28], "int32"), "up32": ("sbuf", [128, 56], "int32"), "snd32": ("sbuf", [128, 12], "int32"),
     "qsb": ("sbuf", [128, C], "bfloat16"), "rmb": ("sbuf", [128, C], "bfloat16"), "cob": ("sbuf", [128, 2 * C], "bfloat16"),
     "scb": ("sbuf", [128, 16], "bfloat16"), "scf": ("sbuf", [128, 16], "float32"),
-    "seq16": ("sbuf", [128, 28], "uint16"), "snd16": ("sbuf", [128, 12], "uint16"), "up16": ("sbuf", [128, 56], "uint16"),
-    "lst2": ("sbuf", [128, 12], "uint16"), "idx16": ("sbuf", [128, 20], "uint16"), "ups16": ("sbuf", [128, 20], "uint16"),
-    "rmp": ("sbuf", [128, C], "float32"), "cr": ("sbuf", [128, 2 * C], "float32"), "crs": ("sbuf", [128, NL], "float32"),
-    "base0": ("sbuf", [128, WIN], "float32"), "base1": ("sbuf", [128, WIN], "float32"),
-    "bs0": ("sbuf", [128, 160], "float32"), "bs1": ("sbuf", [128, 160], "float32"),
+    "seq16": ("sbuf", [128, 28], "uint16"), "up16": ("sbuf", [128, 56], "uint16"), "upr16": ("sbuf", [128, 56], "uint16"),
+    "rmp": ("sbuf", [128, C], "float32"), "cr": ("sbuf", [128, CR * W], "float32"), "z0": ("sbuf", [128, F], "float32"),
     "win0": ("sbuf", [128, WIN], "float32"), "win1": ("sbuf", [128, WIN], "float32"),
-    "psic0": ("sbuf", [128, C], "float32"), "psic1": ("sbuf", [128, C], "float32"), "src": ("sbuf", [128, C], "float32"),
-    "dbl": ("sbuf", [128, 264], "float32"), "dbs": ("sbuf", [128, 136], "float32"),
-    "sco": ("sbuf", [128, 136], "float32"), "scs": ("sbuf", [128, 64], "float32"),
-    "ia": ("sbuf", [128, 56], "int32"), "ib": ("sbuf", [128, 56], "int32"),
-    "ft": ("sbuf", [128, 56], "float32"), "fz": ("sbuf", [128, 56], "float32"), "fa": ("sbuf", [128, 56], "float32"),
-    "fb": ("sbuf", [128, 56], "float32"), "fx": ("sbuf", [128, 56], "float32"), "fy": ("sbuf", [128, 56], "float32"),
-    "fv": ("sbuf", [128, 56], "float32"), "upm": ("sbuf", [128, 56], "float32"),
-    "kk": ("sbuf", [128, 20], "float32"), "kl": ("sbuf", [128, 12], "float32"), "x20": ("sbuf", [128, 20], "float32"),
-    "sa": ("sbuf", [128, 12], "float32"), "saf": ("sbuf", [128, 12], "float32"), "la": ("sbuf", [128, 12], "float32"),
-    "lb": ("sbuf", [128, 12], "float32"), "upd": ("sbuf", [128, 20], "float32"),
-    "iot": ("sbuf", [128, NL], "int32"), "iam": ("sbuf", [128, NL], "int32"), "mskw": ("sbuf", [128, NL], "float32"),
-    "ones": ("sbuf", [128, 128], "float32"), "blk0": ("sbuf", [128, 128], "float32"), "blk": ("sbuf", [128, 128], "float32"),
-    "um": ("sbuf", [128, NX], "float32"), "upf": ("sbuf", [128, NX + 8], "float32"), "upx": ("sbuf", [128, NL], "float32"),
-    "cum": ("sbuf", [128, NL + 16], "float32"), "screp": ("sbuf", [128, 128], "float32"),
-    "yf": ("sbuf", [128, C], "float32"), "yo": ("sbuf", [128, C], "float32"),
+    "psic0": ("sbuf", [128, 512], "float32"), "psic1": ("sbuf", [128, 512], "float32"), "src": ("sbuf", [128, 512], "float32"),
+    "dbs": ("sbuf", [128, 200], "float32"), "ebs": ("sbuf", [128, 200], "float32"),
+    "tab": ("sbuf", [128, Z + 8], "float32"), "zer": ("sbuf", [128, 304], "float32"), "neg": ("sbuf", [128, 200], "float32"),
+    "iot": ("sbuf", [128, 128], "int32"), "iam": ("sbuf", [128, 128], "int32"), "mskw": ("sbuf", [128, 128], "float32"),
+    "pi": ("sbuf", [128, 4], "int32"), "p7": ("sbuf", [128, 4], "int32"), "p8": ("sbuf", [128, 4], "int32"),
+    "ph": ("sbuf", [128, 4], "float32"), "pv": ("sbuf", [128, 4], "float32"), "k18": ("sbuf", [128, 18], "float32"),
+    "pa": ("sbuf", [128, 2], "float32"), "pb": ("sbuf", [128, 2], "float32"), "pl": ("sbuf", [128, 2], "uint16"),
+    "uH": ("sbuf", [128, 48], "int32"), "uL": ("sbuf", [128, 48], "int32"), "ut": ("sbuf", [128, 48], "int32"),
+    "s1": ("sbuf", [128, 12], "float32"), "s2": ("sbuf", [128, 12], "float32"), "s3": ("sbuf", [128, 12], "float32"),
+    "s5": ("sbuf", [128, 12], "float32"), "s6": ("sbuf", [128, 12], "float32"), "s7": ("sbuf", [128, 12], "float32"),
+    "l0": ("sbuf", [128, 2], "uint16"), "l1": ("sbuf", [128, 2], "uint16"),
+    "l96f": ("sbuf", [128, 18], "float32"), "l96g": ("sbuf", [128, 18], "float32"), "l96": ("sbuf", [128, 18], "uint16"),
+    "fo": ("sbuf", [128, 64], "float32"), "cum": ("sbuf", [128, 80], "float32"), "r4": ("sbuf", [128, 4], "float32"),
+    "fo2": ("sbuf", [128, 64], "float32"), "cum2": ("sbuf", [128, 80], "float32"), "r42": ("sbuf", [128, 4], "float32"),
+    "screp": ("sbuf", [128, 128], "float32"), "yo": ("sbuf", [128, 128], "float32"),
+    "qa": ("sbuf", [128, 28], "int32"), "qb": ("sbuf", [128, 28], "int32"), "qc": ("sbuf", [128, 28], "int32"),
+    "qd": ("sbuf", [128, 28], "float32"), "qe": ("sbuf", [128, 28], "float32"), "qf": ("sbuf", [128, 28], "float32"),
+    "qg": ("sbuf", [128, 28], "float32"), "seqp": ("sbuf", [128, 28], "uint16"),
     "ps": ("psum", [128, 2048], "float32"), "pf": ("psum", [128, 2048], "float32"),
 }
-for _s in range(SW):
-    for _w in range(W - 1):
-        SCRATCH["sb%d_%d" % (_s, _w)] = ("sbuf", [128, NS], "float32")
-SEMAPHORES = (["x%d" % i for i in range(NXS)] + ["arr%d_%d" % (s, w) for s in range(SW) for w in range(W - 1)]
-              + ["q_v", "q_s", "q_t", "q_g", "sent"])
+for _n in ("ua", "ub", "uc", "ud", "ue", "uf", "ug", "uh", "ui", "uj", "uk", "um", "un", "uo"):
+    SCRATCH[_n] = ("sbuf", [128, 48], "float32")
+for _i in range(4):
+    SCRATCH["dbl%d" % _i] = ("sbuf", [128, 392], "float32")
+for _k in FULL:
+    SCRATCH["sb%d_%d" % _k] = ("sbuf", [128, 96], "float32")
+for _k in PLAIN:
+    SCRATCH["sb%d_%d" % _k] = ("sbuf", [128, 4 * PLAIN[_k]], "float32")
+for _x in PAIRS:
+    SCRATCH["upf%d" % _x] = ("sbuf", [128, CR], "float32")
+    SCRATCH["ix%d" % _x] = ("sbuf", [128, 4], "uint16")
+    SCRATCH["bx%d" % _x] = ("sbuf", [128, 2], "uint16")
+    SCRATCH["px%d" % _x] = ("sbuf", [128, 4], "uint16")
+    SCRATCH["ex%d" % _x] = ("sbuf", [128, 4], "uint16")
+    SCRATCH["sp%d" % _x] = ("sbuf", [128, 128], "float32")
+    SCRATCH["pk%d" % _x] = ("sbuf", [128, 96], "float32")
+    SCRATCH["lp%d" % _x] = ("sbuf", [128, 128], "float32")
+    SCRATCH["ce%d" % _x] = ("sbuf", [128, 128], "float32")
+SEMAPHORES = (["x%d" % i for i in range(NXS)] + ["arr%d_%d" % k for k in sorted(FULL | set(PLAIN))]
+              + ["pre%d" % x for x in PAIRS] + ["q_%s%d" % (q, i) for q in KQ for i in range(KQ[q])] + ["sent"])
 PSUM = ("ps", "pf")
 
 
@@ -78,17 +104,19 @@ def rank_program(g, core, T, topo):
     cores = list(T.cores)
     others = [c for c in cores if c != core]
     queues = {"v": g.vector, "s": g.scalar, "t": g.tensor, "g": g, "y": g.sync}
-    ops = []
+    ops, group, groups = [], [None], [0]
 
-    def reg(name, a, b):
-        if name in PSUM:
-            return (name, a // 512 * 512, (b + 511) // 512 * 512)
-        return (name, a, b)
+    def together(on):
+        groups[0] += 1
+        group[0] = groups[0] if on else None
+
+    def reg(name, a, b, step=1):
+        return (name, a, b, step)
 
     def R(name, a, b, step=1, p=128):
         t = T[name]
         ap = t[0:p, a:b] if step == 1 else t[0:p, a:b:step]
-        return (ap, [reg(name, a, b)])
+        return (ap, [reg(name, a, b, step)])
 
     def X(name, b, off, oa, ob, a=0):
         return (T[name][:, a:b].indirect(T[off][:, oa:ob]), [reg(name, a, b), reg(off, oa, ob)])
@@ -99,7 +127,7 @@ def rank_program(g, core, T, topo):
             rd += x
         for x in writes:
             wr += x
-        ops.append({"q": q, "fn": fn, "r": rd, "w": wr, "kind": kind, "n": n, "sem": sem})
+        ops.append({"q": q, "fn": fn, "r": rd, "w": wr, "kind": kind, "n": n, "sem": sem, "grp": group[0]})
 
     def split(out):
         return [out[1][0:1]], [out[1][1:]]
@@ -125,14 +153,23 @@ def rank_program(g, core, T, topo):
         add_op("v", lambda: g.vector.tensor_tensor_scan(out=out[0], data0=d0[0], data1=d1[0], initial=0.0, op0=op0, op1=op1),
                [d0[1], d1[1]], [out[1]])
 
-    def act(out, a, scale=None):
-        if scale is None:
-            add_op("s", lambda: g.scalar.activation(out=out[0], in_=a[0], func=AF.Identity), [a[1]], [out[1]])
-        else:
-            add_op("s", lambda: g.scalar.activation(out=out[0], in_=a[0], func=AF.Identity, scale=scale[0]), [a[1], scale[1]], [out[1]])
+    def act(out, a, bias=0.0):
+        add_op("s", lambda: g.scalar.activation(out=out[0], in_=a[0], func=AF.Identity, bias=bias), [a[1]], [out[1]])
 
-    def mm(out, lhsT, rhs):
-        add_op("t", lambda: g.tensor.matmul(out=out[0], lhsT=lhsT[0], rhs=rhs[0], start=True, stop=True), [lhsT[1], rhs[1]], [out[1]])
+    def relu(out, a, bias):
+        add_op("s", lambda: g.scalar.activation(out=out[0], in_=a[0], func=AF.Relu, bias=bias), [a[1]], [out[1]])
+
+    def zeros(name, a, b, step=1):
+        act(R(name, a, b, step), R("zer", 0, len(range(a, b, step))))
+
+    def negs(name, a, b, step=1):
+        act(R(name, a, b, step), R("neg", 0, len(range(a, b, step))))
+
+    def mm(out, lhsT, rhs, start=True, stop=True):
+        add_op("t", lambda: g.tensor.matmul(out=out[0], lhsT=lhsT[0], rhs=rhs[0], start=start, stop=stop), [lhsT[1], rhs[1]], [out[1]])
+
+    def turn(out, a):
+        add_op("v", lambda: g.vector.transpose(out=out[0], in_=a[0]), [a[1]], [out[1]])
 
     def load(q, name, src, p=128):
         n = SCRATCH[name][1][1]
@@ -145,254 +182,445 @@ def rank_program(g, core, T, topo):
         else:
             add_op("g", lambda: g.iota(out[0], pattern, base, cm), [], [out[1]])
 
-    def keep_if(out, a, pattern, base, cm):
-        add_op("g", lambda: g.affine_select(out[0], a[0], pattern, O.is_ge, 0.0, base, cm), [a[1]], [out[1]])
-
-    def slots(w, q):
-        return HD + BW * w + F + CAP * q
-
-    def send(s, w):
-        sb, win, arr = "sb%d_%d" % (s, w), "win%d" % s, T.sem["arr%d_%d" % (s, w)]
-        a = slots(w, rank)
-
+    def message(sb, width, src_at, dst, dst_at, sem):
         def one(call):
-            if len(call) == 1:
-                d, e = call[0]
-                rid, pid = topo.addr(d)[:2]
-                k = T.rank_of(d)
-                return g.remote_dma(out_ap=T[win][:, a:a + CAP], in_ap=T[sb][:, CAP * k:CAP * k + CAP], remote_sem=arr,
-                                    local_sem=T.sem["sent"], pid=pid, routing_id=rid, dma_engine_mask=sum(1 << x for x in e))
             tr = []
             for d, e in call:
                 rid, pid = topo.addr(d)[:2]
                 k = T.rank_of(d)
-                tr.append(RemoteDMATransfer(dst_ids=[DstId(rid=rid, pnc=pid)], dma_engine_mask=sum(1 << x for x in e),
-                                            remote_sem=arr, src=T[sb][:, CAP * k:CAP * k + CAP], dst=T[win][:, a:a + CAP]))
+                sa, da, m = src_at(k), dst_at(k), sum(1 << x for x in e)
+                if len(call) == 1:
+                    return g.remote_dma(out_ap=T[dst][:, da:da + width], in_ap=T[sb][:, sa:sa + width], remote_sem=T.sem[sem],
+                                        local_sem=T.sem["sent"], pid=pid, routing_id=rid, dma_engine_mask=m)
+                tr.append(RemoteDMATransfer(dst_ids=[DstId(rid=rid, pnc=pid)], dma_engine_mask=m, remote_sem=T.sem[sem],
+                                            src=T[sb][:, sa:sa + width], dst=T[dst][:, da:da + width]))
             return g.remote_dma_fused(tr, local_sem=T.sem["sent"])
 
+        n = SCRATCH[sb][1][1]
         for call in send_calls(topo, core, others):
-            add_op("g", lambda call=call: one(call), [[(sb, 0, NS)]], [], "remote", sum(len(e) for d, e in call))
+            add_op("g", lambda call=call: one(call), [[reg(sb, 0, n)]], [], "remote", sum(len(e) for d, e in call))
+
+    def landing(dst, width, at, sem):
+        n = sum(engines_to(topo, c, core, [d for d in cores if d != c]) for c in others)
+        add_op("ext", None, [], [[reg(dst, at(T.rank_of(c)), at(T.rank_of(c)) + width) for c in others]], "ext", n, sem)
+
+    def index_of(k):
+        return [T.rank_of(c) for c in others].index(k)
+
+    def plain_at(w, s, d):
+        if w % 2 == 0:
+            return slot_at(w) + 32 * s + 8 * d
+        return slot_at(w) + 32 + 24 * s
+
+    def send(s, w):
+        sb, win, sem = "sb%d_%d" % (s, w), "win%d" % s, "arr%d_%d" % (s, w)
+        if (s, w) in FULL:
+            message(sb, NS, lambda k: NS * index_of(k), win, lambda k: slot_at(w) + NS * rank, sem)
+            act(R(win, slot_at(w) + NS * rank, slot_at(w) + NS * rank + NS), R(sb, 0, NS))
+        else:
+            c = PLAIN[(s, w)]
+            message(sb, c, lambda k: c * k, win, lambda k: plain_at(w, rank, k), sem)
 
     def arrival(s, w):
-        n = sum(engines_to(topo, c, core, [d for d in cores if d != c]) for c in others)
-        wr = [("win%d" % s, slots(w, T.rank_of(c)), slots(w, T.rank_of(c)) + CAP) for c in others]
-        add_op("ext", None, [], [wr], "ext", n, "arr%d_%d" % (s, w))
+        win, sem = "win%d" % s, "arr%d_%d" % (s, w)
+        if (s, w) in FULL:
+            landing(win, NS, lambda k: slot_at(w) + NS * k, sem)
+        else:
+            landing(win, PLAIN[(s, w)], lambda k: plain_at(w, k, rank), sem)
 
     def own(s, w):
-        return R("win%d" % s, HD + BW * w, HD + BW * w + F)
+        return R("win%d" % s, own_at(w) + 2, own_at(w) + 192, 3)
 
-    def chain(s, w):
-        tt(R("dbl", 1, 257, 2), X("win%d" % s, HD + BW * w, "up16", 8 * w, 8 * w + 8), R("cr", 128 * w, 128 * w + 128), O.mult)
-        scan(R("sco", 0, 128), R("dbl", 0, 128), R("dbl", 129, 257), O.add, O.max)
+    def chain_gather(s, w):
+        tt(R("dbl%d" % (w % 4), 1, 385, 3), X("win%d" % s, own_at(w), "up16", 8 * w, 8 * w + 8), R("cr", CR * w, CR * w + 128), O.mult)
 
-    def finish(s, w):
-        tt(own(s, w), R("sco", 1, 128, 2), R("base%d" % s, F * w, F * w + F), O.add)
+    def chain_scan(s, w):
+        d = "dbl%d" % (w % 4)
+        scan(R("win%d" % s, own_at(w), own_at(w) + 192), R(d, 0, 192), R(d, 193, 385), O.add, O.max)
 
-    def to_cells(s, w):
-        cp(X("psic%d" % s, C, "seq16", 4 * w, 4 * w + 4), own(s, w))
+    def finish_gather(s, x):
+        w = x - 1
+        act(R("ebs", 2, 98, 3), X("win%d" % s, slot_at(w) + 128, "pl", 0, 2, slot_at(w)))
+        tt(R("ebs", 1, 193, 3), X("win%d" % s, slot_at(w) + 128, "ex%d" % x, 0, 4, slot_at(w) - 8), R("ce%d" % x, 64, 128), O.mult)
 
-    def send_first(s, w):
-        tt(R("dbs", 1, 129, 2), X("win%d" % s, HD + BW * w, "ups16", 4 * (w - 1), 4 * w), R("crs", 64 * (w - 1), 64 * w), O.mult)
-        scan(R("scs", 0, 64), R("dbs", 0, 64), R("dbs", 65, 129), O.add, O.max)
-        tt(R("sb%d_%d" % (s, w), 0, NS), R("scs", 1, 64, 2), R("bs%d" % s, NS * (w - 1), NS * w), O.add)
+    def finish_scan(s, x):
+        a = slot_at(x) + 32
+        scan(R("win%d" % s, a, a + 96), R("ebs", 0, 96), R("ebs", 97, 193), O.add, O.max)
+
+    def partial_base(x):
+        cp(R("dbs", 2, 98, 3), X("dbl%d" % (x % 4), 392, "bx%d" % x, 0, 2))
+
+    def partial(s, w):
+        x, win, i = w + 1, "win%d" % s, w // 2
+        tt(R("dbs", 1, 193, 3), X(win, own_at(w) + 200, "px%d" % x, 0, 4), R("sp%d" % x, 64, 128), O.mult)
+        scan(R(win, 8, 104), R("dbs", 0, 96), R("dbs", 97, 193), O.add, O.max)
+        cp(R("sb%d_%d" % (s, w), 0, 96), X(win, own_at(w) + 200, "l96", 6 * i, 6 * i + 6))
         send(s, w)
 
-    def prep(s, w):
-        ts(R("dbl", 130, 258, 2), R("base%d" % s, F * w, F * w + F), -1.0, O.mult)
+    def base(w, src):
+        x = X("qsb", C, "seq16", 4 * w, 4 * w + 4) if src == "qsb" else X("src", 512, "seqp", 4 * w, 4 * w + 4)
+        tt(R("dbl%d" % (w % 4), 2, 194, 3), x, R("rmp", F * w, F * w + F), O.mult)
 
-    def prep_first(s, w):
-        ts(R("dbs", 66, 130, 2), R("bs%d" % s, NS * (w - 1), NS * w), -1.0, O.mult)
+    def twice_at(w):
+        return 128 * (w - 2) + 512 if 2 <= w < 6 else 128 * (w == 6) * 8
+
+    def twice(w):
+        for u in range(U):
+            act(R("ps", twice_at(w) + 64 * u, twice_at(w) + 64 * u + F), R("rmp", F * w, F * w + F))
 
     def coef(w):
+        tt(R("cr", CR * w, CR * w + 128), R("cob", 128 * w, 128 * w + 128), R("ps", twice_at(w), twice_at(w) + 128), O.mult)
+
+    def to_cells(s, w):
+        cp(X("psic%d" % s, 512, "seqp", 4 * w, 4 * w + 4), own(s, w))
+
+    def flux(s, j, start, stop):
+        mm(R("pf", 512 * j, 512 * j + 32, 1, CELLS[j]), R("psic%d" % s, 128 * j, 128 * j + CELLS[j]), R("mskw", 0, 32), start, stop)
+
+    def spread(x):
+        act(R("upf%d" % x, 0, 128), X("tab", Z + 8, "upr16", 8 * x, 8 * x + 8))
+
+    def picks(x):
         for u in range(U):
-            a = 128 * w + 64 * u
-            tt(R("cr", a, a + F), R("cob", a, a + F), R("rmp", F * w, F * w + F), O.mult)
+            ts(R("ix%d" % x, 2 * u, 2 * u + 2), R("s2", 2 * x, 2 * x + 2), float(64 * u - 64 * x), O.add, 128.0, O.min)
+        ts(R("bx%d" % x, 0, 2), R("s3", 2 * x, 2 * x + 2), float(2 - 192 * x), O.add, 195.0, O.min)
 
-    def send_base(s, a, b):
-        cp(R("bs%d" % s, NS * (a - 1), NS * (b - 1)), X("base%d" % s, WIN, "snd16", 2 * a, 2 * b))
+    def cells_sent(x):
+        act(R("sp%d" % x, 0, 64), X("upf%d" % x, CR, "ix%d" % x, 0, 4))
+        act(R("sp%d" % x, 64, 128), X("cr", CR * x + CR, "ix%d" % x, 0, 4, CR * x))
 
-    def self_slots(s):
-        for w in range(W - 1):
-            fill(R("win%d" % s, slots(w, rank), slots(w, rank) + CAP), 0.0)
+    def fold(src, out, limit, op, t):
+        tt(R("fo" + t, 0, 64), R(src, 0, 64), R("mskw", 0, 64), O.mult)
+        scan(R("cum" + t, 16, 80), R("fo" + t, 0, 64), R("fo" + t, 0, 64), O.add, O.max)
+        tt(R("r4" + t, 0, 4), R("cum" + t, 31, 80, 16), R("cum" + t, 15, 64, 16), O.subtract)
+        ts(R(out, 0, 4), R("r4" + t, 0, 4), *([limit, O.min] if op == "min" else [limit, O.max, -limit, O.add]))
+
+    def pack(x):
+        together(True)
+        for c in others:
+            k, i = T.rank_of(c), index_of(T.rank_of(c))
+            for j in range(4):
+                act(R("pk%d" % x, 32 * i + 8 * j, 32 * i + 8 * j + 8), R("sp%d" % x, 32 * j + 8 * k, 32 * j + 8 * k + 8))
+        together(False)
+        message("pk%d" % x, NS, lambda k: NS * index_of(k), "lp%d" % x, lambda k: NS * rank, "pre%d" % x)
+
+    def unpack(x):
+        landing("lp%d" % x, NS, lambda k: NS * k, "pre%d" % x)
+        together(True)
+        for c in others:
+            k = T.rank_of(c)
+            for j in range(4):
+                act(R("ce%d" % x, 32 * j + 8 * k, 32 * j + 8 * k + 8), R("lp%d" % x, 32 * k + 8 * j, 32 * k + 8 * j + 8))
+        together(False)
+
+    def known(x):
+        fold("sp%d" % x, "px%d" % x, float(slot_at(x - 1) - 1), "min", "")
+
+    def unknown(x):
+        fold("ce%d" % x, "ex%d" % x, float(slot_at(x - 1) - 8), "max", "2")
 
     load("y", "seq32", T.seq)
+    load("s", "snd32", T.snd)
     load("s", "rmb", T.rm)
     load("y", "qsb", T.qs)
-    load("s", "snd32", T.snd)
     load("y", "up32", T.up)
     load("s", "cob", T.co)
     load("y", "scb", T.sc, 16)
-    iota(R("iot", 0, NL), [[1, NL]], 1024, -1, False)
-    fill(R("ones", 0, 128), 1.0)
-    fill(R("base0", 0, WIN), 0.0)
-    fill(R("dbl", 0, 264), -BIG)
-    fill(R("dbs", 0, 136), -BIG)
-    fill(R("win0", 0, HD), 0.0)
-    iota(R("kl", 0, 12), [[-128, 6], [0, 2]], 0, 0, True)
-    iota(R("kk", 0, 20), [[64, 5], [64, 2], [0, 2]], -64, 0, True)
-    keep_if(R("blk0", 0, 128), R("ones", 0, 128), [[-16, 8], [0, 16]], 0, 1)
-    keep_if(R("blk", 0, 128), R("blk0", 0, 128), [[16, 8], [0, 16]], 15, -1)
-    ts(R("iam", 0, NL), R("iot", 0, NL), 15, O.bitwise_and)
-    ts(R("mskw", 0, NL), R("iam", 0, NL), 0.0, O.is_equal)
+    iota(R("pi", 0, 4), [[0, 4]], 0, 1, False)
+    iota(R("iot", 0, 128), [[1, 128]], 1024, -1, False)
+    iota(R("tab", 0, 64), [[3, 64]], own_at(0) + 2, 0, True)
+    iota(R("tab", C, C + 32), [[32, 4], [1, 8]], slot_at(0) + 8 * rank, 0, True)
+    iota(R("tab", C + 32, C + 64), [[3, 32]], slot_at(1) + 34, 0, True)
+    fill(R("zer", 0, 304), 0.0)
+    fill(R("neg", 0, 200), -BIG)
+    together(True)
+    zeros("win0", 0, own_at(0) + 200)
+    for s in range(NR):
+        a = slot_at(0) + NS * s
+        if s == rank:
+            zeros("win0", a, a + NS)
+        else:
+            if rank > 0:
+                zeros("win0", a, a + 8 * rank)
+            if rank < NR - 1:
+                zeros("win0", a + 8 * rank + 8, a + NS)
+    together(False)
+    together(True)
+    zeros("sb0_1", 0, 96)
+    zeros("win0", slot_at(1) - 8, slot_at(1) + 32)
+    zeros("win0", slot_at(1) + 32 + 24 * rank, slot_at(1) + 56 + 24 * rank)
+    for i in (1, 2):
+        negs("dbl%d" % i, 0, 192, 3)
+        negs("dbl%d" % i, 194, 386, 3)
+        zeros("dbl%d" % i, 195, 387, 3)
+    together(False)
+    ts(R("p7", 0, 4), R("pi", 0, 4), 7, O.bitwise_and)
+    ts(R("p8", 0, 4), R("pi", 0, 4), 8, O.bitwise_and)
+    ts(R("iam", 0, 128), R("iot", 0, 128), 15, O.bitwise_and)
+    fill(R("k18", 0, 18), 0.0)
+    ts(R("mskw", 0, 128), R("iam", 0, 128), 0.0, O.is_equal)
 
     cp(R("seq16", 0, 28), R("seq32", 0, 28))
+    ts(R("s5", 0, 12), R("snd32", 0, 12), float(Z), O.is_ge, -8192.0, O.mult)
+    ts(R("s6", 0, 12), R("snd32", 0, 12), 3.0, O.mult)
     cp(R("rmp", 0, F), X("rmb", C, "seq16", 0, 4))
-    cp(R("snd16", 0, 12), R("snd32", 0, 12))
-    tt(R("base0", 0, F), X("qsb", C, "seq16", 0, 4), R("rmp", 0, F), O.mult)
-    ts(R("sb0_0", 0, NS), X("base0", WIN, "snd16", 0, 2), 0.0, O.max)
+    tt(R("s7", 0, 12), R("s6", 0, 12), R("s5", 0, 12), O.add)
+    tt(R("z0", 0, F), X("qsb", C, "seq16", 0, 4), R("rmp", 0, F), O.mult)
+    ts(R("l0", 0, 2), R("s7", 0, 2), float(own_at(0) + 2), O.add, 0.0, O.max)
+    ts(own(0, 0), R("z0", 0, F), 0.0, O.max)
+    cp(R("sb0_0", 0, NS), X("win0", own_at(0) + 200, "l0", 0, 2))
     send(0, 0)
     act(R("rmp", F, C), X("rmb", C, "seq16", 4, 28))
-    ts(R("ia", 0, 56), R("up32", 0, 56), 0x3C0, O.bitwise_and)
-    ts(R("ib", 0, 56), R("up32", 0, 56), 0x3E0, O.bitwise_and)
-    ts(R("ft", 0, 56), R("up32", 0, 56), float(C), O.is_ge, -4096.0, O.mult)
-    ts(R("fz", 0, 56), R("up32", 0, 56), float(Z), O.is_ge, -648.0, O.mult)
-    ts(R("fa", 0, 56), R("ia", 0, 56), 0.5, O.mult, 8.0, O.add)
-    ts(R("fb", 0, 56), R("ib", 0, 56), 2.0, O.mult, -1272.0, O.add)
-    tt(R("fv", 0, 56), R("up32", 0, 56), R("fz", 0, 56), O.add)
-    tt(R("fx", 0, 56), R("fa", 0, 56), R("ft", 0, 56), O.add)
-    tt(R("fy", 0, 56), R("fx", 0, 56), R("fb", 0, 56), O.max)
-    tt(R("upm", 0, 56), R("fy", 0, 56), R("fv", 0, 56), O.add)
-    cp(R("up16", 0, 56), R("upm", 0, 56))
-    ts(own(0, 0), R("base0", 0, F), 0.0, O.max)
-    tt(R("base0", F, 2 * F), X("qsb", C, "seq16", 4, 8), R("rmp", F, 2 * F), O.mult)
-    prep(0, 1)
+    together(True)
+    twice(1)
+    together(False)
+    together(True)
+    for w in range(2, W):
+        twice(w)
+    together(False)
+    u, fu = R("up32", 8, 56), (lambda n: R(n, 0, 48))
+    shift = OFF - 266.0
+    ts(fu("uH"), u, 0x3C0, O.bitwise_and)
+    ts(fu("uL"), u, 0x3F, O.bitwise_and)
+    ts(fu("ut"), u, 7, O.bitwise_and)
+    ts(fu("ud"), u, float(C), O.is_ge, -8192.0, O.mult)
+    ts(fu("un"), u, float(Z), O.is_ge, -8192.0, O.mult)
+    ts(fu("ua"), fu("uH"), 5.125, O.mult, float(own_at(0) + 2), O.add)
+    ts(fu("ub"), fu("uL"), 3.0, O.mult)
+    ts(fu("ue"), fu("uH"), 10.25, O.mult, float(slot_at(0)) - 10.25 * C - shift, O.add)
+    ts(fu("uf"), fu("uL"), 4.0, O.mult, 8.0 * rank + shift, O.add)
+    ts(fu("ug"), fu("ut"), 3.0, O.mult)
+    ts(fu("ui"), fu("uL"), 32.0, O.is_ge, OFF, O.mult)
+    tt(fu("uc"), fu("ua"), fu("ub"), O.add)
+    tt(fu("uh"), fu("uf"), fu("ug"), O.subtract)
+    tt(fu("uj"), fu("ub"), fu("ui"), O.add)
+    tt(fu("uo"), fu("ue"), fu("un"), O.add)
+    tt(fu("um"), fu("uc"), fu("ud"), O.add)
+    tt(fu("uk"), fu("uh"), fu("uj"), O.max)
+    base(1, "qsb")
+    tt(fu("ue"), fu("uo"), fu("uk"), O.add)
     coef(1)
-    ts(R("la", 0, 12), R("snd32", 0, 12), 2.0, O.mult, 1.0, O.add)
-    tt(R("lb", 0, 12), R("la", 0, 12), R("kl", 0, 12), O.add)
-    ts(R("lst2", 0, 12), R("lb", 0, 12), 128.0, O.min)
-    fill(R("sco", 128, 136), 0.0)
-    self_slots(0)
-    send_base(0, 1, 2)
-    for i in range(16):
-        act(R("um", i, NX, 16), R("upm", 8, 48), R("mskw", i, i + 1))
-    mm(R("ps", 0, 320), R("blk", 0, 128), R("um", 0, 320))
-    mm(R("ps", 512, 832), R("blk", 0, 128), R("um", 320, 640))
-    act(R("upf", 0, 320), R("ps", 0, 320))
-    act(R("upf", 320, 640), R("ps", 512, 832))
+    tt(fu("ua"), fu("um"), fu("ue"), O.max)
+    ts(R("l1", 0, 2), R("s7", 2, 4), float(own_at(1) + 2 - 192), O.add, 0.0, O.max)
+    cp(R("up16", 8, 56), fu("ua"))
+    ts(R("s1", 0, 12), R("snd32", 0, 12), float(Z), O.is_ge, 1024.0, O.mult)
+    cp(R("upr16", 0, 56), R("up32", 0, 56))
+    tt(R("s2", 0, 12), R("snd32", 0, 12), R("s1", 0, 12), O.add)
+    ts(R("s3", 0, 12), R("s2", 0, 12), 3.0, O.mult)
+    picks(3)
+    together(True)
+    for i in range(3):
+        for j in range(3):
+            a = 6 * i + 2 * j
+            relu(R("l96f", a, a + 2), R("s7", 4 * i, 4 * i + 2), float(own_at(2 * i) + 2 - 384 * i))
+    together(False)
+    together(True)
+    for i in range(1, W):
+        act(R("tab", 64 * i, 64 * i + 64), R("tab", 0, 64), float(BW * i))
+    for i in range(2, W - 1):
+        a, b = C + 32 * i, C + 32 * (i % 2)
+        act(R("tab", a, a + 32), R("tab", b, b + 32), float(BW * (i - i % 2)))
+    zeros("tab", Z, Z + 8)
+    zeros("upf3", 128, CR)
+    zeros("cr", CR * 3 + 128, CR * 4)
+    together(False)
+    together(True)
+    negs("dbl3", 0, 192, 3)
+    negs("dbl3", 194, 386, 3)
+    zeros("dbl3", 195, 387, 3)
+    negs("dbs", 0, 200)
+    zeros("cum", 0, 16)
+    together(False)
     arrival(0, 0)
 
-    for w in range(1, W):
-        last = w == W - 1
-        if w < DUP:
-            chain(0, w)
-            tt(R("sb0_%d" % w, 0, NS), X("sco", 136, "lst2", 2 * w, 2 * w + 2), R("bs0", NS * (w - 1), NS * w), O.add)
-            send(0, w)
-            finish(0, w)
-        elif not last:
-            send_first(0, w)
-            chain(0, w)
-            finish(0, w)
-        else:
-            chain(0, w)
-            tt(X("psic0", C, "seq16", 4 * w, 4 * w + 4), R("sco", 1, 128, 2), R("base0", F * w, F * w + F), O.add)
-        if w == 1:
-            tt(R("base0", 2 * F, C), X("qsb", C, "seq16", 8, 28), R("rmp", 2 * F, C), O.mult)
-            prep(0, 2)
-            coef(2)
-            send_base(0, 2, 6)
-            fill(R("upf", NX, NX + 8), 0.0)
-            fill(R("cum", 0, 16), 0.0)
-            fill(R("cr", 128 + NX, 128 + NX + 8), 0.0)
-            ts(R("sa", 0, 12), R("snd32", 0, 12), float(Z), O.is_ge, 512.0, O.mult)
-            tt(R("saf", 0, 12), R("snd32", 0, 12), R("sa", 0, 12), O.add)
-            for u in range(U):
-                for c in range(2):
-                    tt(R("x20", 2 * u + c, 20, 4), R("saf", 2 + c, 12, 2), R("kk", 2 * u + c, 20, 4), O.add)
-            ts(R("idx16", 0, 20), R("x20", 0, 20), float(NX), O.min)
-            for x in range(3, W - 1):
-                coef(x)
-        if w == 2:
-            prep(0, 3)
-            tt(R("upx", 0, NL), X("upf", NX + 8, "idx16", 0, 20), R("mskw", 0, NL), O.mult)
-            scan(R("cum", 16, NL + 16), R("upx", 0, NL), R("upx", 0, NL), O.add, O.max)
-            tt(R("upd", 0, 20), R("cum", 31, NL + 16, 16), R("cum", 15, NL, 16), O.subtract)
-            cp(R("ups16", 0, 20), R("upd", 0, 20))
-            cp(R("crs", 0, NL), X("cr", 128 + NX + 8, "idx16", 0, 20, 128))
-            prep_first(0, 3)
-        if w == 3:
-            coef(6)
-        if 3 <= w < W - 1:
-            prep(0, w + 1)
-            if w + 1 < W - 1:
-                prep_first(0, w + 1)
-        if w == 3:
-            for x in range(3):
-                to_cells(0, x)
-        if 3 <= w < W - 1:
-            to_cells(0, w)
-        if w == 4:
-            fill(R("base1", 0, WIN), 0.0)
-            fill(R("win1", 0, HD), 0.0)
-            cp(R("scf", 0, 16, 1, 16), R("scb", 0, 16, 1, 16))
-            mm(R("pf", 0, 16), R("mskw", 0, 128, 1, 16), R("scf", 0, 16, 1, 16))
-            for i in range(8):
-                act(R("screp", 16 * i, 16 * i + 16), R("pf", 0, 16))
-        if w == 5:
-            self_slots(1)
-        if not last:
-            arrival(0, w)
+    chain_gather(0, 1)
+    chain_scan(0, 1)
+    cp(R("sb0_1", 2, 96, 3), X("win0", own_at(1) + 200, "l1", 0, 2))
+    send(0, 1)
+    coef(3)
+    spread(3)
+    cells_sent(3)
+    pack(3)
+    base(2, "qsb")
+    together(True)
+    negs("dbl0", 0, 192, 3)
+    negs("dbl0", 194, 386, 3)
+    zeros("dbl0", 195, 387, 3)
+    for i in range(2, W - 1):
+        zeros("win0", slot_at(i) - 8, slot_at(i) + (32 if i % 2 else 0))
+    for x in PAIRS:
+        zeros("ce%d" % x, 0, 128)
+    negs("ebs", 0, 97)
+    negs("ebs", 98, 194, 3)
+    zeros("ebs", 99, 195, 3)
+    zeros("cum2", 0, 16)
+    for x in (5, 1):
+        zeros("upf%d" % x, 128, CR)
+        zeros("cr", CR * x + 128, CR * (x + 1))
+    zeros("src", 352, 512)
+    together(False)
+    coef(2)
+    base(3, "qsb")
+    ts(R("ph", 0, 3), R("p8", 0, 3), float(8 * (rank % 2)), O.is_equal)
+    ts(R("pv", 0, 3), R("p7", 0, 3), 3.0, O.mult)
+    ts(R("pa", 0, 2), R("p8", 0, 2), 5.0, O.mult)
+    partial_base(3)
+    for c in others:
+        k, i = T.rank_of(c), index_of(T.rank_of(c))
+        a = 2 * i + rank // 2
+        o, v, h = R("k18", a, a + 13, 6), R("pv", 0, 3), R("ph", 0, 1)
+        add_op("v", lambda o=o, v=v, h=h, k=k: g.vector.tensor_scalar(out=o[0], in0=v[0], scalar1=float(24 * k + 10), scalar2=h[0],
+                                                                      op0=O.add, op1=O.mult), [v[1], h[1]], [o[1]])
+    known(3)
+    tt(R("l96g", 0, 18), R("l96f", 0, 18), R("k18", 0, 18), O.add)
+    tt(R("pb", 0, 2), R("pa", 0, 2), R("p7", 0, 2), O.add)
+    cp(R("l96", 0, 18), R("l96g", 0, 18))
+    ts(R("qa", 0, 28), R("seq32", 0, 28), 0x1F, O.bitwise_and)
+    ts(R("qb", 0, 28), R("seq32", 0, 28), 0x60, O.bitwise_and)
+    ts(R("qc", 0, 28), R("seq32", 0, 28), 0x180, O.bitwise_and)
+    arrival(0, 1)
 
-    for i in range(CH):
-        mm(R("ps", 512 * i, 512 * i + CW), R("screp", 0, 128), R("psic0", CW * i, CW * i + CW))
-    for i in range(CH):
-        o, a = R("src", CW * i, CW * i + CW), R("ps", 512 * i, 512 * i + CW)
+    chain_gather(0, 2)
+    chain_scan(0, 2)
+    partial(0, 2)
+    spread(5)
+    unpack(3)
+    picks(5)
+    coef(5)
+    cells_sent(5)
+    pack(5)
+    ts(R("pl", 0, 1), R("pb", 0, 1), 0.0, O.add)
+    ts(R("pl", 1, 2), R("pb", 1, 2), 80.0, O.add)
+    base(4, "qsb")
+    coef(4)
+    base(5, "qsb")
+    unknown(3)
+    partial_base(5)
+    known(5)
+    arrival(0, 2)
+
+    finish_gather(0, 3)
+    chain_gather(0, 3)
+    finish_scan(0, 3)
+    chain_scan(0, 3)
+    chain_gather(0, 4)
+    chain_scan(0, 4)
+    partial(0, 4)
+    unpack(5)
+    spread(1)
+    picks(1)
+    cells_sent(1)
+    pack(1)
+    ts(R("qd", 0, 28), R("qb", 0, 28), 4.0, O.mult)
+    ts(R("qe", 0, 28), R("qc", 0, 28), 0.25, O.mult)
+    base(6, "qsb")
+    tt(R("qf", 0, 28), R("qd", 0, 28), R("qa", 0, 28), O.add)
+    coef(6)
+    tt(R("qg", 0, 28), R("qf", 0, 28), R("qe", 0, 28), O.add)
+    unknown(5)
+    cp(R("seqp", 0, 28), R("qg", 0, 28))
+    for x in range(3):
+        to_cells(0, x)
+    zeros("win1", 0, own_at(0) + 200)
+    arrival(0, 4)
+
+    finish_gather(0, 5)
+    chain_gather(0, 5)
+    finish_scan(0, 5)
+    chain_scan(0, 5)
+    chain_gather(0, 6)
+    cp(R("scf", 0, 16, 1, 16), R("scb", 0, 16, 1, 16))
+    mm(R("pf", 0, 16), R("mskw", 0, 128, 1, 16), R("scf", 0, 16, 1, 16))
+    together(True)
+    for i in range(8):
+        act(R("screp", 16 * i, 16 * i + 16), R("pf", 0, 16))
+    together(False)
+    chain_scan(0, 6)
+    for x in (3, 4, 5, 6):
+        to_cells(0, x)
+
+    for i in range(4):
+        mm(R("ps", 512 * i, 512 * i + CELLS[i]), R("screp", 0, 128), R("psic0", 128 * i, 128 * i + CELLS[i]))
+    known(1)
+    for i in range(4):
+        o, a = R("src", 128 * i, 128 * i + CELLS[i]), R("ps", 512 * i, 512 * i + CELLS[i])
         if i % 2 == 0:
             act(o, a)
         else:
             cp(o, a)
-    tt(R("base1", 0, F), X("src", C, "seq16", 0, 4), R("rmp", 0, F), O.mult)
-    ts(R("sb1_0", 0, NS), X("base1", WIN, "snd16", 0, 2), 0.0, O.max)
-    send(1, 0)
-    for i in range(CH):
-        mm(R("pf", 512 * i, 512 * i + CW, 1, 16), R("mskw", 0, 16), R("psic0", CW * i, CW * i + CW))
-    for i in range(CH):
-        act(R("yf", CW * i, CW * i + CW, 1, 16), R("pf", 512 * i, 512 * i + CW, 1, 16))
-    ts(own(1, 0), R("base1", 0, F), 0.0, O.max)
-    tt(R("base1", F, C), X("src", C, "seq16", 4, 28), R("rmp", F, C), O.mult)
-    send_base(1, 1, 6)
-    prep_first(1, 1)
-    prep(1, 1)
+    tt(R("z0", 0, F), X("src", 512, "seqp", 0, 4), R("rmp", 0, F), O.mult)
+    base(1, "src")
+    ts(own(1, 0), R("z0", 0, F), 0.0, O.max)
+    partial_base(1)
+    partial(1, 0)
+    unpack(1)
+    together(True)
+    for i in range(1, W - 1):
+        zeros("win1", slot_at(i) - 8, slot_at(i) + (32 if i % 2 else 0))
+    together(False)
+    for j in range(4):
+        flux(0, j, True, False)
+    base(2, "src")
+    base(3, "src")
     to_cells(1, 0)
+    partial_base(3)
+    unknown(1)
     arrival(1, 0)
 
-    for w in range(1, W):
-        if w < W - 1:
-            send_first(1, w)
-            chain(1, w)
-            finish(1, w)
-            prep(1, w + 1)
-            if w + 1 < W - 1:
-                prep_first(1, w + 1)
-            to_cells(1, w)
-            arrival(1, w)
+    for x in (1, 3, 5):
+        finish_gather(1, x)
+        chain_gather(1, x)
+        finish_scan(1, x)
+        chain_scan(1, x)
+        chain_gather(1, x + 1)
+        chain_scan(1, x + 1)
+        if x < 5:
+            partial(1, x + 1)
+            base(x + 3, "src")
+            if x == 1:
+                base(5, "src")
+                partial_base(5)
+            to_cells(1, x)
+            to_cells(1, x + 1)
+            arrival(1, x + 1)
         else:
-            chain(1, w)
-            tt(X("psic1", C, "seq16", 4 * w, 4 * w + 4), R("sco", 1, 128, 2), R("base1", F * w, F * w + F), O.add)
+            to_cells(1, 5)
+            to_cells(1, 6)
 
-    for i in range(CH):
-        mm(R("pf", 512 * i, 512 * i + CW, 1, 16), R("mskw", 0, 16), R("psic1", CW * i, CW * i + CW))
-    for i in range(CH):
-        a, b = CW * i, CW * i + CW
-        tt(R("yo", a, b, 1, 16), R("pf", 512 * i, 512 * i + CW, 1, 16), R("yf", a, b, 1, 16), O.add)
-        q = "y" if i % 2 == 1 else "s"
-        add_op(q, lambda q=q, a=a, b=b: queues[q].dma_start(T.y[:, a:b], T.yo[0:16, a:b]), [[("yo", a, b)]], [[("y", a, b)]], "dma", 16)
+    for j in range(4):
+        flux(1, j, False, True)
+    for j in range(4):
+        turn(R("yo", 32 * j, 32 * j + 32, 1, CELLS[j]), R("pf", 512 * j, 512 * j + 32, 1, CELLS[j]))
+    for k in range(4):
+        a, b = 128 * k, min(C, 128 * k + 128)
+        q = "y" if k % 2 == 1 else "s"
+        add_op(q, lambda q=q, a=a, b=b, k=k: queues[q].dma_start(T.y[:, a:b], T.yo[32 * k:32 * k + 16, 0:b - a]),
+               [[("yo", 0, b - a, 1)]], [[("y", a, b, 1)]], "dma", 16)
 
     emit(g, T, queues, ops)
+
+
+def meets(x, y, same):
+    if x[0] in PSUM and x[0] == y[0] and not same:
+        return x[1] // 512 <= (y[2] - 1) // 512 and y[1] // 512 <= (x[2] - 1) // 512
+    if x[0] != y[0] or x[1] >= y[2] or y[1] >= x[2]:
+        return False
+    return x[3] != y[3] or x[3] == 1 or (x[1] - y[1]) % x[3] == 0
 
 
 def clash(a, b):
     for x in a["w"]:
         for y in b["r"] + b["w"]:
-            if x[0] == y[0] and x[1] < y[2] and y[1] < x[2]:
+            if meets(x, y, a["q"] == b["q"]):
                 return True
     for x in a["r"]:
         for y in b["w"] + (b["r"] if x[0] in PSUM and a["q"] != b["q"] else []):
-            if x[0] == y[0] and x[1] < y[2] and y[1] < x[2]:
+            if meets(x, y, a["q"] == b["q"]):
                 return True
     return False
 
 
-def plan_waits(ops, flagged):
+def plan_waits(ops, flagged, members):
     known, issued, start, waits, new = {}, {}, {}, [], set(flagged)
     for i, o in enumerate(ops):
         ws = []
@@ -402,7 +630,7 @@ def plan_waits(ops, flagged):
             waits.append(ws)
             continue
         k = known.get(q, 0)
-        mine = issued.setdefault(q, [])
+        mine = issued.setdefault(q, [[] for r in range(KQ.get(q, 1))])
         for j in range(i - 1, -1, -1):
             if k >> j & 1 or not clash(o, ops[j]):
                 continue
@@ -410,35 +638,47 @@ def plan_waits(ops, flagged):
             if p["kind"] == "remote":
                 raise ValueError("a call waits for a message's source")
             if p["q"] == q and p["kind"] == "c" and j not in flagged:
-                ws.append(("q", len(mine)))
-                for m in mine:
+                r = [n for n in range(len(mine)) if j in mine[n]][0]
+                ws.append(("q", (r, len(mine[r]))))
+                for m in mine[r]:
                     k |= 1 << m | start[m]
             else:
-                ws.append(("u", j))
-                k |= 1 << j | start[j]
+                all_of = members.get(p["grp"], [j])
+                if all_of[-1] >= i:
+                    raise ValueError("a call waits for a group that isn't whole yet")
+                ws.append(("u", all_of[0]))
+                for m in all_of:
+                    k |= 1 << m | start[m]
                 if p["kind"] == "c":
-                    new.add(j)
+                    new.update(all_of)
         start[i] = k
         known[q] = k
         if o["kind"] == "c" and i not in flagged:
-            mine.append(i)
+            mine[sum(len(m) for m in mine) % len(mine)].append(i)
         waits.append(ws)
     return waits, new
 
 
 def emit(g, T, queues, ops):
-    flagged = set()
+    flagged, members, names = set(), {}, {}
+    for i, o in enumerate(ops):
+        if o["grp"] is not None and o["kind"] == "c":
+            members.setdefault(o["grp"], []).append(i)
     while True:
-        waits, new = plan_waits(ops, flagged)
+        waits, new = plan_waits(ops, flagged, members)
         if new == flagged:
             break
         flagged = new
-    names = {}
+    own, total = 0, {}
     for i, o in enumerate(ops):
+        first = members.get(o["grp"], [i])[0]
         if o["kind"] == "ext":
-            names[i] = o["sem"]
+            names[i], total[i] = o["sem"], o["n"]
+        elif first in names:
+            names[i] = names[first]
         elif o["kind"] == "dma" or i in flagged:
-            names[i] = "x%d" % len([k for k in names if names[k][0] == "x"])
+            names[i], total[i] = "x%d" % own, o["n"] * len(members.get(o["grp"], [i]))
+            own += 1
     count, done, sent, waited = {}, {}, 0, set()
     for i, o in enumerate(ops):
         if o["kind"] == "ext":
@@ -446,10 +686,10 @@ def emit(g, T, queues, ops):
         q = o["q"]
         for kind, v in waits[i]:
             if kind == "q":
-                queues[q].wait_ge(T.sem["q_" + q], v)
-                done[q] = v
+                queues[q].wait_ge(T.sem["q_%s%d" % (q, v[0])], v[1])
+                done[(q, v[0])] = v[1]
             else:
-                queues[q].wait_ge(T.sem[names[v]], ops[v]["n"])
+                queues[q].wait_ge(T.sem[names[v]], total[v])
                 waited.add(v)
         x = o["fn"]()
         if o["kind"] == "remote":
@@ -457,12 +697,13 @@ def emit(g, T, queues, ops):
         elif i in names:
             x.then_inc(T.sem[names[i]], o["n"])
         else:
-            x.then_inc(T.sem["q_" + q], 1)
-            count[q] = count.get(q, 0) + 1
-    for q in count:
-        if done.get(q, 0) < count[q]:
-            queues[q].wait_ge(T.sem["q_" + q], count[q])
+            r = sum(count.get((q, n), 0) for n in range(KQ[q])) % KQ[q]
+            x.then_inc(T.sem["q_%s%d" % (q, r)], 1)
+            count[(q, r)] = count.get((q, r), 0) + 1
+    for q, r in count:
+        if done.get((q, r), 0) < count[(q, r)]:
+            queues[q].wait_ge(T.sem["q_%s%d" % (q, r)], count[(q, r)])
     g.wait_ge(T.sem["sent"], sent)
-    for i, o in enumerate(ops):
-        if i in names and i not in waited:
-            queues[o["q"]].wait_ge(T.sem[names[i]], o["n"])
+    for i in total:
+        if i not in waited:
+            queues[ops[i]["q"]].wait_ge(T.sem[names[i]], total[i])

from concourse.bass import DstId, RemoteDMATransfer
from concourse.mybir import AluOpType as O, ActivationFunctionType as AF

W, F, U, CAP, SW, NR = 7, 64, 2, 8, 2, 4
C = W * F
Z = C + (W - 1) * NR * CAP
NS = NR * CAP
BW = 328
HD = 104
WIN = HD + BW * (W - 1) + 192
CR = 136
BIG = 9.0e29
OFF = 4096.0
CELLS = (128, 128, 96, 96)
KQ = {"v": 8, "s": 8, "t": 2, "g": 2}
NXS = 108
FULL = {(0, 2), (0, 4), (1, 0), (1, 2), (1, 4)}
PLAIN = {(0, 0): CAP, (0, 1): 3 * CAP}
PAIRS = (3, 5, 1)


def own_at(w):
    return HD + BW * w


def slot_at(w):
    return HD + BW * w + 200


SCRATCH = {
    "seq32": ("sbuf", [128, 28], "int32"), "up32": ("sbuf", [128, 56], "int32"), "snd32": ("sbuf", [128, 12], "int32"),
    "qsb": ("sbuf", [128, C], "bfloat16"), "rmb": ("sbuf", [128, C], "bfloat16"), "cob": ("sbuf", [128, 2 * C], "bfloat16"),
    "scb": ("sbuf", [128, 16], "bfloat16"), "scf": ("sbuf", [128, 16], "float32"),
    "seq16": ("sbuf", [128, 28], "uint16"), "up16": ("sbuf", [128, 56], "uint16"), "upr16": ("sbuf", [128, 56], "uint16"),
    "rmp": ("sbuf", [128, C], "float32"), "cr": ("sbuf", [128, CR * W], "float32"), "z0": ("sbuf", [128, F], "float32"),
    "win0": ("sbuf", [128, WIN], "float32"), "win1": ("sbuf", [128, WIN], "float32"),
    "psic0": ("sbuf", [128, 512], "float32"), "psic1": ("sbuf", [128, 512], "float32"), "src": ("sbuf", [128, 512], "float32"),
    "dbs": ("sbuf", [128, 200], "float32"), "ebs": ("sbuf", [128, 200], "float32"),
    "tab": ("sbuf", [128, Z + 8], "float32"), "zer": ("sbuf", [128, 304], "float32"), "neg": ("sbuf", [128, 200], "float32"),
    "iot": ("sbuf", [128, 128], "int32"), "iam": ("sbuf", [128, 128], "int32"), "mskw": ("sbuf", [128, 128], "float32"),
    "pi": ("sbuf", [128, 4], "int32"), "p7": ("sbuf", [128, 4], "int32"), "p8": ("sbuf", [128, 4], "int32"),
    "ph": ("sbuf", [128, 4], "float32"), "pv": ("sbuf", [128, 4], "float32"), "k18": ("sbuf", [128, 18], "float32"),
    "pa": ("sbuf", [128, 2], "float32"), "pb": ("sbuf", [128, 2], "float32"), "pl": ("sbuf", [128, 2], "uint16"),
    "uH": ("sbuf", [128, 48], "int32"), "uL": ("sbuf", [128, 48], "int32"), "ut": ("sbuf", [128, 48], "int32"),
    "s1": ("sbuf", [128, 12], "float32"), "s2": ("sbuf", [128, 12], "float32"), "s3": ("sbuf", [128, 12], "float32"),
    "s5": ("sbuf", [128, 12], "float32"), "s6": ("sbuf", [128, 12], "float32"), "s7": ("sbuf", [128, 12], "float32"),
    "l0": ("sbuf", [128, 2], "uint16"), "l1": ("sbuf", [128, 2], "uint16"),
    "l96f": ("sbuf", [128, 18], "float32"), "l96g": ("sbuf", [128, 18], "float32"), "l96": ("sbuf", [128, 18], "uint16"),
    "fo": ("sbuf", [128, 64], "float32"), "cum": ("sbuf", [128, 80], "float32"), "r4": ("sbuf", [128, 4], "float32"),
    "fo2": ("sbuf", [128, 64], "float32"), "cum2": ("sbuf", [128, 80], "float32"), "r42": ("sbuf", [128, 4], "float32"),
    "screp": ("sbuf", [128, 128], "float32"), "yo": ("sbuf", [128, 128], "float32"),
    "qa": ("sbuf", [128, 28], "int32"), "qb": ("sbuf", [128, 28], "int32"), "qc": ("sbuf", [128, 28], "int32"),
    "qd": ("sbuf", [128, 28], "float32"), "qe": ("sbuf", [128, 28], "float32"), "qf": ("sbuf", [128, 28], "float32"),
    "qg": ("sbuf", [128, 28], "float32"), "seqp": ("sbuf", [128, 28], "uint16"),
    "ps": ("psum", [128, 2048], "float32"), "pf": ("psum", [128, 2048], "float32"),
}
for _n in ("ua", "ub", "uc", "ud", "ue", "uf", "ug", "uh", "ui", "uj", "uk", "um", "un", "uo"):
    SCRATCH[_n] = ("sbuf", [128, 48], "float32")
for _i in range(4):
    SCRATCH["dbl%d" % _i] = ("sbuf", [128, 392], "float32")
for _k in FULL:
    SCRATCH["sb%d_%d" % _k] = ("sbuf", [128, 96], "float32")
for _k in PLAIN:
    SCRATCH["sb%d_%d" % _k] = ("sbuf", [128, 4 * PLAIN[_k]], "float32")
for _x in PAIRS:
    SCRATCH["upf%d" % _x] = ("sbuf", [128, CR], "float32")
    SCRATCH["ix%d" % _x] = ("sbuf", [128, 4], "uint16")
    SCRATCH["bx%d" % _x] = ("sbuf", [128, 2], "uint16")
    SCRATCH["px%d" % _x] = ("sbuf", [128, 4], "uint16")
    SCRATCH["ex%d" % _x] = ("sbuf", [128, 4], "uint16")
    SCRATCH["sp%d" % _x] = ("sbuf", [128, 128], "float32")
    SCRATCH["pk%d" % _x] = ("sbuf", [128, 96], "float32")
    SCRATCH["lp%d" % _x] = ("sbuf", [128, 128], "float32")
    SCRATCH["ce%d" % _x] = ("sbuf", [128, 128], "float32")
SEMAPHORES = (["x%d" % i for i in range(NXS)] + ["arr%d_%d" % k for k in sorted(FULL | set(PLAIN))]
              + ["pre%d" % x for x in PAIRS] + ["q_%s%d" % (q, i) for q in KQ for i in range(KQ[q])] + ["sent"])
PSUM = ("ps", "pf")


def send_calls(topo, src, dests):
    far = [d for d in dests if not topo.mates(topo.chip(src), topo.chip(d))]
    near = [d for d in dests if topo.mates(topo.chip(src), topo.chip(d))]
    far.sort(key=lambda d: topo.same_plane(topo.chip(src), topo.chip(d)))
    calls = []
    if len(far) == 2 and len(near) == 1:
        e = [topo.engines(src, d) for d in far]
        h = len(e[0]) // 2
        calls.append([(far[0], e[0][:h]), (far[1], e[1][h:])])
        calls.append([(near[0], topo.engines(src, near[0]))])
    else:
        for d in far + near:
            calls.append([(d, topo.engines(src, d))])
    return calls


def engines_to(topo, src, dst, dests):
    return sum(len(e) for call in send_calls(topo, src, dests) for d, e in call if d == dst)


def rank_program(g, core, T, topo):
    rank = T.rank_of(core)
    if rank is None:
        return
    cores = list(T.cores)
    others = [c for c in cores if c != core]
    queues = {"v": g.vector, "s": g.scalar, "t": g.tensor, "g": g, "y": g.sync}
    ops, group, groups = [], [None], [0]

    def together(on):
        groups[0] += 1
        group[0] = groups[0] if on else None

    def reg(name, a, b, step=1):
        return (name, a, b, step)

    def R(name, a, b, step=1, p=128):
        t = T[name]
        ap = t[0:p, a:b] if step == 1 else t[0:p, a:b:step]
        return (ap, [reg(name, a, b, step)])

    def X(name, b, off, oa, ob, a=0):
        return (T[name][:, a:b].indirect(T[off][:, oa:ob]), [reg(name, a, b), reg(off, oa, ob)])

    def add_op(q, fn, reads, writes, kind="c", n=1, sem=None):
        rd, wr = [], []
        for x in reads:
            rd += x
        for x in writes:
            wr += x
        ops.append({"q": q, "fn": fn, "r": rd, "w": wr, "kind": kind, "n": n, "sem": sem, "grp": group[0]})

    def split(out):
        return [out[1][0:1]], [out[1][1:]]

    def tt(out, a, b, op):
        w, r = split(out)
        add_op("v", lambda: g.vector.tensor_tensor(out=out[0], in0=a[0], in1=b[0], op=op), [a[1], b[1]] + r, w)

    def ts(out, a, s1, op0, s2=None, op1=None):
        if op1 is None:
            add_op("v", lambda: g.vector.tensor_scalar(out=out[0], in0=a[0], scalar1=s1, scalar2=None, op0=op0), [a[1]], [out[1]])
        else:
            add_op("v", lambda: g.vector.tensor_scalar(out=out[0], in0=a[0], scalar1=s1, scalar2=s2, op0=op0, op1=op1), [a[1]], [out[1]])

    def cp(out, a):
        w, r = split(out)
        add_op("v", lambda: g.vector.tensor_copy(out=out[0], in_=a[0]), [a[1]] + r, w)

    def fill(out, v):
        add_op("v", lambda: g.vector.memset(out[0], v), [], [out[1]])

    def scan(out, d0, d1, op0, op1):
        add_op("v", lambda: g.vector.tensor_tensor_scan(out=out[0], data0=d0[0], data1=d1[0], initial=0.0, op0=op0, op1=op1),
               [d0[1], d1[1]], [out[1]])

    def act(out, a, bias=0.0):
        add_op("s", lambda: g.scalar.activation(out=out[0], in_=a[0], func=AF.Identity, bias=bias), [a[1]], [out[1]])

    def relu(out, a, bias):
        add_op("s", lambda: g.scalar.activation(out=out[0], in_=a[0], func=AF.Relu, bias=bias), [a[1]], [out[1]])

    def zeros(name, a, b, step=1):
        act(R(name, a, b, step), R("zer", 0, len(range(a, b, step))))

    def negs(name, a, b, step=1):
        act(R(name, a, b, step), R("neg", 0, len(range(a, b, step))))

    def mm(out, lhsT, rhs, start=True, stop=True):
        add_op("t", lambda: g.tensor.matmul(out=out[0], lhsT=lhsT[0], rhs=rhs[0], start=start, stop=stop), [lhsT[1], rhs[1]], [out[1]])

    def turn(out, a):
        add_op("v", lambda: g.vector.transpose(out=out[0], in_=a[0]), [a[1]], [out[1]])

    def load(q, name, src, p=128):
        n = SCRATCH[name][1][1]
        o = R(name, 0, n, 1, p)
        add_op(q, lambda: queues[q].dma_start(o[0], src[:, :]), [], [o[1]], "dma", 16)

    def iota(out, pattern, base, cm, flag):
        if flag:
            add_op("g", lambda: g.iota(out[0], pattern, base, cm, allow_small_or_imprecise_dtypes=True), [], [out[1]])
        else:
            add_op("g", lambda: g.iota(out[0], pattern, base, cm), [], [out[1]])

    def message(sb, width, src_at, dst, dst_at, sem):
        def one(call):
            tr = []
            for d, e in call:
                rid, pid = topo.addr(d)[:2]
                k = T.rank_of(d)
                sa, da, m = src_at(k), dst_at(k), sum(1 << x for x in e)
                if len(call) == 1:
                    return g.remote_dma(out_ap=T[dst][:, da:da + width], in_ap=T[sb][:, sa:sa + width], remote_sem=T.sem[sem],
                                        local_sem=T.sem["sent"], pid=pid, routing_id=rid, dma_engine_mask=m)
                tr.append(RemoteDMATransfer(dst_ids=[DstId(rid=rid, pnc=pid)], dma_engine_mask=m, remote_sem=T.sem[sem],
                                            src=T[sb][:, sa:sa + width], dst=T[dst][:, da:da + width]))
            return g.remote_dma_fused(tr, local_sem=T.sem["sent"])

        n = SCRATCH[sb][1][1]
        for call in send_calls(topo, core, others):
            add_op("g", lambda call=call: one(call), [[reg(sb, 0, n)]], [], "remote", sum(len(e) for d, e in call))

    def landing(dst, width, at, sem):
        n = sum(engines_to(topo, c, core, [d for d in cores if d != c]) for c in others)
        add_op("ext", None, [], [[reg(dst, at(T.rank_of(c)), at(T.rank_of(c)) + width) for c in others]], "ext", n, sem)

    def index_of(k):
        return [T.rank_of(c) for c in others].index(k)

    def plain_at(w, s, d):
        if w % 2 == 0:
            return slot_at(w) + 32 * s + 8 * d
        return slot_at(w) + 32 + 24 * s

    def send(s, w):
        sb, win, sem = "sb%d_%d" % (s, w), "win%d" % s, "arr%d_%d" % (s, w)
        if (s, w) in FULL:
            message(sb, NS, lambda k: NS * index_of(k), win, lambda k: slot_at(w) + NS * rank, sem)
            act(R(win, slot_at(w) + NS * rank, slot_at(w) + NS * rank + NS), R(sb, 0, NS))
        else:
            c = PLAIN[(s, w)]
            message(sb, c, lambda k: c * k, win, lambda k: plain_at(w, rank, k), sem)

    def arrival(s, w):
        win, sem = "win%d" % s, "arr%d_%d" % (s, w)
        if (s, w) in FULL:
            landing(win, NS, lambda k: slot_at(w) + NS * k, sem)
        else:
            landing(win, PLAIN[(s, w)], lambda k: plain_at(w, k, rank), sem)

    def own(s, w):
        return R("win%d" % s, own_at(w) + 2, own_at(w) + 192, 3)

    def chain_gather(s, w):
        tt(R("dbl%d" % (w % 4), 1, 385, 3), X("win%d" % s, own_at(w), "up16", 8 * w, 8 * w + 8), R("cr", CR * w, CR * w + 128), O.mult)

    def chain_scan(s, w):
        d = "dbl%d" % (w % 4)
        scan(R("win%d" % s, own_at(w), own_at(w) + 192), R(d, 0, 192), R(d, 193, 385), O.add, O.max)

    def finish_gather(s, x):
        w = x - 1
        act(R("ebs", 2, 98, 3), X("win%d" % s, slot_at(w) + 128, "pl", 0, 2, slot_at(w)))
        tt(R("ebs", 1, 193, 3), X("win%d" % s, slot_at(w) + 128, "ex%d" % x, 0, 4, slot_at(w) - 8), R("ce%d" % x, 64, 128), O.mult)

    def finish_scan(s, x):
        a = slot_at(x) + 32
        scan(R("win%d" % s, a, a + 96), R("ebs", 0, 96), R("ebs", 97, 193), O.add, O.max)

    def partial_base(x):
        cp(R("dbs", 2, 98, 3), X("dbl%d" % (x % 4), 392, "bx%d" % x, 0, 2))

    def partial(s, w):
        x, win, i = w + 1, "win%d" % s, w // 2
        tt(R("dbs", 1, 193, 3), X(win, own_at(w) + 200, "px%d" % x, 0, 4), R("sp%d" % x, 64, 128), O.mult)
        scan(R(win, 8, 104), R("dbs", 0, 96), R("dbs", 97, 193), O.add, O.max)
        cp(R("sb%d_%d" % (s, w), 0, 96), X(win, own_at(w) + 200, "l96", 6 * i, 6 * i + 6))
        send(s, w)

    def base(w, src):
        x = X("qsb", C, "seq16", 4 * w, 4 * w + 4) if src == "qsb" else X("src", 512, "seqp", 4 * w, 4 * w + 4)
        tt(R("dbl%d" % (w % 4), 2, 194, 3), x, R("rmp", F * w, F * w + F), O.mult)

    def twice_at(w):
        return 128 * (w - 2) + 512 if 2 <= w < 6 else 128 * (w == 6) * 8

    def twice(w):
        for u in range(U):
            act(R("ps", twice_at(w) + 64 * u, twice_at(w) + 64 * u + F), R("rmp", F * w, F * w + F))

    def coef(w):
        tt(R("cr", CR * w, CR * w + 128), R("cob", 128 * w, 128 * w + 128), R("ps", twice_at(w), twice_at(w) + 128), O.mult)

    def to_cells(s, w):
        cp(X("psic%d" % s, 512, "seqp", 4 * w, 4 * w + 4), own(s, w))

    def flux(s, j, start, stop):
        mm(R("pf", 512 * j, 512 * j + 32, 1, CELLS[j]), R("psic%d" % s, 128 * j, 128 * j + CELLS[j]), R("mskw", 0, 32), start, stop)

    def spread(x):
        act(R("upf%d" % x, 0, 128), X("tab", Z + 8, "upr16", 8 * x, 8 * x + 8))

    def picks(x):
        for u in range(U):
            ts(R("ix%d" % x, 2 * u, 2 * u + 2), R("s2", 2 * x, 2 * x + 2), float(64 * u - 64 * x), O.add, 128.0, O.min)
        ts(R("bx%d" % x, 0, 2), R("s3", 2 * x, 2 * x + 2), float(2 - 192 * x), O.add, 195.0, O.min)

    def cells_sent(x):
        act(R("sp%d" % x, 0, 64), X("upf%d" % x, CR, "ix%d" % x, 0, 4))
        act(R("sp%d" % x, 64, 128), X("cr", CR * x + CR, "ix%d" % x, 0, 4, CR * x))

    def fold(src, out, limit, op, t):
        tt(R("fo" + t, 0, 64), R(src, 0, 64), R("mskw", 0, 64), O.mult)
        scan(R("cum" + t, 16, 80), R("fo" + t, 0, 64), R("fo" + t, 0, 64), O.add, O.max)
        tt(R("r4" + t, 0, 4), R("cum" + t, 31, 80, 16), R("cum" + t, 15, 64, 16), O.subtract)
        ts(R(out, 0, 4), R("r4" + t, 0, 4), *([limit, O.min] if op == "min" else [limit, O.max, -limit, O.add]))

    def pack(x):
        together(True)
        for c in others:
            k, i = T.rank_of(c), index_of(T.rank_of(c))
            for j in range(4):
                act(R("pk%d" % x, 32 * i + 8 * j, 32 * i + 8 * j + 8), R("sp%d" % x, 32 * j + 8 * k, 32 * j + 8 * k + 8))
        together(False)
        message("pk%d" % x, NS, lambda k: NS * index_of(k), "lp%d" % x, lambda k: NS * rank, "pre%d" % x)

    def unpack(x):
        landing("lp%d" % x, NS, lambda k: NS * k, "pre%d" % x)
        together(True)
        for c in others:
            k = T.rank_of(c)
            for j in range(4):
                act(R("ce%d" % x, 32 * j + 8 * k, 32 * j + 8 * k + 8), R("lp%d" % x, 32 * k + 8 * j, 32 * k + 8 * j + 8))
        together(False)

    def known(x):
        fold("sp%d" % x, "px%d" % x, float(slot_at(x - 1) - 1), "min", "")

    def unknown(x):
        fold("ce%d" % x, "ex%d" % x, float(slot_at(x - 1) - 8), "max", "2")

    load("y", "seq32", T.seq)
    load("s", "snd32", T.snd)
    load("s", "rmb", T.rm)
    load("y", "qsb", T.qs)
    load("y", "up32", T.up)
    load("s", "cob", T.co)
    load("y", "scb", T.sc, 16)
    iota(R("pi", 0, 4), [[0, 4]], 0, 1, False)
    iota(R("iot", 0, 128), [[1, 128]], 1024, -1, False)
    iota(R("tab", 0, 64), [[3, 64]], own_at(0) + 2, 0, True)
    iota(R("tab", C, C + 32), [[32, 4], [1, 8]], slot_at(0) + 8 * rank, 0, True)
    iota(R("tab", C + 32, C + 64), [[3, 32]], slot_at(1) + 34, 0, True)
    fill(R("zer", 0, 304), 0.0)
    fill(R("neg", 0, 200), -BIG)
    together(True)
    zeros("win0", 0, own_at(0) + 200)
    for s in range(NR):
        a = slot_at(0) + NS * s
        if s == rank:
            zeros("win0", a, a + NS)
        else:
            if rank > 0:
                zeros("win0", a, a + 8 * rank)
            if rank < NR - 1:
                zeros("win0", a + 8 * rank + 8, a + NS)
    together(False)
    together(True)
    zeros("sb0_1", 0, 96)
    zeros("win0", slot_at(1) - 8, slot_at(1) + 32)
    zeros("win0", slot_at(1) + 32 + 24 * rank, slot_at(1) + 56 + 24 * rank)
    for i in (1, 2):
        negs("dbl%d" % i, 0, 192, 3)
        negs("dbl%d" % i, 194, 386, 3)
        zeros("dbl%d" % i, 195, 387, 3)
    together(False)
    ts(R("p7", 0, 4), R("pi", 0, 4), 7, O.bitwise_and)
    ts(R("p8", 0, 4), R("pi", 0, 4), 8, O.bitwise_and)
    ts(R("iam", 0, 128), R("iot", 0, 128), 15, O.bitwise_and)
    fill(R("k18", 0, 18), 0.0)
    ts(R("mskw", 0, 128), R("iam", 0, 128), 0.0, O.is_equal)

    cp(R("seq16", 0, 28), R("seq32", 0, 28))
    ts(R("s5", 0, 12), R("snd32", 0, 12), float(Z), O.is_ge, -8192.0, O.mult)
    ts(R("s6", 0, 12), R("snd32", 0, 12), 3.0, O.mult)
    cp(R("rmp", 0, F), X("rmb", C, "seq16", 0, 4))
    tt(R("s7", 0, 12), R("s6", 0, 12), R("s5", 0, 12), O.add)
    tt(R("z0", 0, F), X("qsb", C, "seq16", 0, 4), R("rmp", 0, F), O.mult)
    ts(R("l0", 0, 2), R("s7", 0, 2), float(own_at(0) + 2), O.add, 0.0, O.max)
    ts(own(0, 0), R("z0", 0, F), 0.0, O.max)
    cp(R("sb0_0", 0, NS), X("win0", own_at(0) + 200, "l0", 0, 2))
    send(0, 0)
    act(R("rmp", F, C), X("rmb", C, "seq16", 4, 28))
    together(True)
    twice(1)
    together(False)
    together(True)
    for w in range(2, W):
        twice(w)
    together(False)
    u, fu = R("up32", 8, 56), (lambda n: R(n, 0, 48))
    shift = OFF - 266.0
    ts(fu("uH"), u, 0x3C0, O.bitwise_and)
    ts(fu("uL"), u, 0x3F, O.bitwise_and)
    ts(fu("ut"), u, 7, O.bitwise_and)
    ts(fu("ud"), u, float(C), O.is_ge, -8192.0, O.mult)
    ts(fu("un"), u, float(Z), O.is_ge, -8192.0, O.mult)
    ts(fu("ua"), fu("uH"), 5.125, O.mult, float(own_at(0) + 2), O.add)
    ts(fu("ub"), fu("uL"), 3.0, O.mult)
    ts(fu("ue"), fu("uH"), 10.25, O.mult, float(slot_at(0)) - 10.25 * C - shift, O.add)
    ts(fu("uf"), fu("uL"), 4.0, O.mult, 8.0 * rank + shift, O.add)
    ts(fu("ug"), fu("ut"), 3.0, O.mult)
    ts(fu("ui"), fu("uL"), 32.0, O.is_ge, OFF, O.mult)
    tt(fu("uc"), fu("ua"), fu("ub"), O.add)
    tt(fu("uh"), fu("uf"), fu("ug"), O.subtract)
    tt(fu("uj"), fu("ub"), fu("ui"), O.add)
    tt(fu("uo"), fu("ue"), fu("un"), O.add)
    tt(fu("um"), fu("uc"), fu("ud"), O.add)
    tt(fu("uk"), fu("uh"), fu("uj"), O.max)
    base(1, "qsb")
    tt(fu("ue"), fu("uo"), fu("uk"), O.add)
    coef(1)
    tt(fu("ua"), fu("um"), fu("ue"), O.max)
    ts(R("l1", 0, 2), R("s7", 2, 4), float(own_at(1) + 2 - 192), O.add, 0.0, O.max)
    cp(R("up16", 8, 56), fu("ua"))
    ts(R("s1", 0, 12), R("snd32", 0, 12), float(Z), O.is_ge, 1024.0, O.mult)
    cp(R("upr16", 0, 56), R("up32", 0, 56))
    tt(R("s2", 0, 12), R("snd32", 0, 12), R("s1", 0, 12), O.add)
    ts(R("s3", 0, 12), R("s2", 0, 12), 3.0, O.mult)
    picks(3)
    together(True)
    for i in range(3):
        for j in range(3):
            a = 6 * i + 2 * j
            relu(R("l96f", a, a + 2), R("s7", 4 * i, 4 * i + 2), float(own_at(2 * i) + 2 - 384 * i))
    together(False)
    together(True)
    for i in range(1, W):
        act(R("tab", 64 * i, 64 * i + 64), R("tab", 0, 64), float(BW * i))
    for i in range(2, W - 1):
        a, b = C + 32 * i, C + 32 * (i % 2)
        act(R("tab", a, a + 32), R("tab", b, b + 32), float(BW * (i - i % 2)))
    zeros("tab", Z, Z + 8)
    zeros("upf3", 128, CR)
    zeros("cr", CR * 3 + 128, CR * 4)
    together(False)
    together(True)
    negs("dbl3", 0, 192, 3)
    negs("dbl3", 194, 386, 3)
    zeros("dbl3", 195, 387, 3)
    negs("dbs", 0, 200)
    zeros("cum", 0, 16)
    together(False)
    arrival(0, 0)

    chain_gather(0, 1)
    chain_scan(0, 1)
    cp(R("sb0_1", 2, 96, 3), X("win0", own_at(1) + 200, "l1", 0, 2))
    send(0, 1)
    coef(3)
    spread(3)
    cells_sent(3)
    pack(3)
    base(2, "qsb")
    together(True)
    negs("dbl0", 0, 192, 3)
    negs("dbl0", 194, 386, 3)
    zeros("dbl0", 195, 387, 3)
    for i in range(2, W - 1):
        zeros("win0", slot_at(i) - 8, slot_at(i) + (32 if i % 2 else 0))
    for x in PAIRS:
        zeros("ce%d" % x, 0, 128)
    negs("ebs", 0, 97)
    negs("ebs", 98, 194, 3)
    zeros("ebs", 99, 195, 3)
    zeros("cum2", 0, 16)
    for x in (5, 1):
        zeros("upf%d" % x, 128, CR)
        zeros("cr", CR * x + 128, CR * (x + 1))
    zeros("src", 352, 512)
    together(False)
    coef(2)
    base(3, "qsb")
    ts(R("ph", 0, 3), R("p8", 0, 3), float(8 * (rank % 2)), O.is_equal)
    ts(R("pv", 0, 3), R("p7", 0, 3), 3.0, O.mult)
    ts(R("pa", 0, 2), R("p8", 0, 2), 5.0, O.mult)
    partial_base(3)
    for c in others:
        k, i = T.rank_of(c), index_of(T.rank_of(c))
        a = 2 * i + rank // 2
        o, v, h = R("k18", a, a + 13, 6), R("pv", 0, 3), R("ph", 0, 1)
        add_op("v", lambda o=o, v=v, h=h, k=k: g.vector.tensor_scalar(out=o[0], in0=v[0], scalar1=float(24 * k + 10), scalar2=h[0],
                                                                      op0=O.add, op1=O.mult), [v[1], h[1]], [o[1]])
    known(3)
    tt(R("l96g", 0, 18), R("l96f", 0, 18), R("k18", 0, 18), O.add)
    tt(R("pb", 0, 2), R("pa", 0, 2), R("p7", 0, 2), O.add)
    cp(R("l96", 0, 18), R("l96g", 0, 18))
    ts(R("qa", 0, 28), R("seq32", 0, 28), 0x1F, O.bitwise_and)
    ts(R("qb", 0, 28), R("seq32", 0, 28), 0x60, O.bitwise_and)
    ts(R("qc", 0, 28), R("seq32", 0, 28), 0x180, O.bitwise_and)
    arrival(0, 1)

    chain_gather(0, 2)
    chain_scan(0, 2)
    partial(0, 2)
    spread(5)
    unpack(3)
    picks(5)
    coef(5)
    cells_sent(5)
    pack(5)
    ts(R("pl", 0, 1), R("pb", 0, 1), 0.0, O.add)
    ts(R("pl", 1, 2), R("pb", 1, 2), 80.0, O.add)
    base(4, "qsb")
    coef(4)
    base(5, "qsb")
    unknown(3)
    partial_base(5)
    known(5)
    arrival(0, 2)

    finish_gather(0, 3)
    chain_gather(0, 3)
    finish_scan(0, 3)
    chain_scan(0, 3)
    chain_gather(0, 4)
    chain_scan(0, 4)
    partial(0, 4)
    unpack(5)
    spread(1)
    picks(1)
    cells_sent(1)
    pack(1)
    ts(R("qd", 0, 28), R("qb", 0, 28), 4.0, O.mult)
    ts(R("qe", 0, 28), R("qc", 0, 28), 0.25, O.mult)
    base(6, "qsb")
    tt(R("qf", 0, 28), R("qd", 0, 28), R("qa", 0, 28), O.add)
    coef(6)
    tt(R("qg", 0, 28), R("qf", 0, 28), R("qe", 0, 28), O.add)
    unknown(5)
    cp(R("seqp", 0, 28), R("qg", 0, 28))
    for x in range(3):
        to_cells(0, x)
    zeros("win1", 0, own_at(0) + 200)
    arrival(0, 4)

    finish_gather(0, 5)
    chain_gather(0, 5)
    finish_scan(0, 5)
    chain_scan(0, 5)
    chain_gather(0, 6)
    cp(R("scf", 0, 16, 1, 16), R("scb", 0, 16, 1, 16))
    mm(R("pf", 0, 16), R("mskw", 0, 128, 1, 16), R("scf", 0, 16, 1, 16))
    together(True)
    for i in range(8):
        act(R("screp", 16 * i, 16 * i + 16), R("pf", 0, 16))
    together(False)
    chain_scan(0, 6)
    for x in (3, 4, 5, 6):
        to_cells(0, x)

    for i in range(4):
        mm(R("ps", 512 * i, 512 * i + CELLS[i]), R("screp", 0, 128), R("psic0", 128 * i, 128 * i + CELLS[i]))
    known(1)
    for i in range(4):
        o, a = R("src", 128 * i, 128 * i + CELLS[i]), R("ps", 512 * i, 512 * i + CELLS[i])
        if i % 2 == 0:
            act(o, a)
        else:
            cp(o, a)
    tt(R("z0", 0, F), X("src", 512, "seqp", 0, 4), R("rmp", 0, F), O.mult)
    base(1, "src")
    ts(own(1, 0), R("z0", 0, F), 0.0, O.max)
    partial_base(1)
    partial(1, 0)
    unpack(1)
    together(True)
    for i in range(1, W - 1):
        zeros("win1", slot_at(i) - 8, slot_at(i) + (32 if i % 2 else 0))
    together(False)
    for j in range(4):
        flux(0, j, True, False)
    base(2, "src")
    base(3, "src")
    to_cells(1, 0)
    partial_base(3)
    unknown(1)
    arrival(1, 0)

    for x in (1, 3, 5):
        finish_gather(1, x)
        chain_gather(1, x)
        finish_scan(1, x)
        chain_scan(1, x)
        chain_gather(1, x + 1)
        chain_scan(1, x + 1)
        if x < 5:
            partial(1, x + 1)
            base(x + 3, "src")
            if x == 1:
                base(5, "src")
                partial_base(5)
            to_cells(1, x)
            to_cells(1, x + 1)
            arrival(1, x + 1)
        else:
            to_cells(1, 5)
            to_cells(1, 6)

    for j in range(4):
        flux(1, j, False, True)
    for j in range(4):
        turn(R("yo", 32 * j, 32 * j + 32, 1, CELLS[j]), R("pf", 512 * j, 512 * j + 32, 1, CELLS[j]))
    for k in range(4):
        a, b = 128 * k, min(C, 128 * k + 128)
        q = "y" if k % 2 == 1 else "s"
        add_op(q, lambda q=q, a=a, b=b, k=k: queues[q].dma_start(T.y[:, a:b], T.yo[32 * k:32 * k + 16, 0:b - a]),
               [[("yo", 0, b - a, 1)]], [[("y", a, b, 1)]], "dma", 16)

    emit(g, T, queues, ops)


def meets(x, y, same):
    if x[0] in PSUM and x[0] == y[0] and not same:
        return x[1] // 512 <= (y[2] - 1) // 512 and y[1] // 512 <= (x[2] - 1) // 512
    if x[0] != y[0] or x[1] >= y[2] or y[1] >= x[2]:
        return False
    return x[3] != y[3] or x[3] == 1 or (x[1] - y[1]) % x[3] == 0


def clash(a, b):
    for x in a["w"]:
        for y in b["r"] + b["w"]:
            if meets(x, y, a["q"] == b["q"]):
                return True
    for x in a["r"]:
        for y in b["w"] + (b["r"] if x[0] in PSUM and a["q"] != b["q"] else []):
            if meets(x, y, a["q"] == b["q"]):
                return True
    return False


def plan_waits(ops, flagged, members):
    known, issued, start, waits, new = {}, {}, {}, [], set(flagged)
    for i, o in enumerate(ops):
        ws = []
        q = o["q"]
        if o["kind"] == "ext":
            start[i] = 0
            waits.append(ws)
            continue
        k = known.get(q, 0)
        mine = issued.setdefault(q, [[] for r in range(KQ.get(q, 1))])
        for j in range(i - 1, -1, -1):
            if k >> j & 1 or not clash(o, ops[j]):
                continue
            p = ops[j]
            if p["kind"] == "remote":
                raise ValueError("a call waits for a message's source")
            if p["q"] == q and p["kind"] == "c" and j not in flagged:
                r = [n for n in range(len(mine)) if j in mine[n]][0]
                ws.append(("q", (r, len(mine[r]))))
                for m in mine[r]:
                    k |= 1 << m | start[m]
            else:
                all_of = members.get(p["grp"], [j])
                if all_of[-1] >= i:
                    raise ValueError("a call waits for a group that isn't whole yet")
                ws.append(("u", all_of[0]))
                for m in all_of:
                    k |= 1 << m | start[m]
                if p["kind"] == "c":
                    new.update(all_of)
        start[i] = k
        known[q] = k
        if o["kind"] == "c" and i not in flagged:
            mine[sum(len(m) for m in mine) % len(mine)].append(i)
        waits.append(ws)
    return waits, new


def emit(g, T, queues, ops):
    flagged, members, names = set(), {}, {}
    for i, o in enumerate(ops):
        if o["grp"] is not None and o["kind"] == "c":
            members.setdefault(o["grp"], []).append(i)
    while True:
        waits, new = plan_waits(ops, flagged, members)
        if new == flagged:
            break
        flagged = new
    own, total = 0, {}
    for i, o in enumerate(ops):
        first = members.get(o["grp"], [i])[0]
        if o["kind"] == "ext":
            names[i], total[i] = o["sem"], o["n"]
        elif first in names:
            names[i] = names[first]
        elif o["kind"] == "dma" or i in flagged:
            names[i], total[i] = "x%d" % own, o["n"] * len(members.get(o["grp"], [i]))
            own += 1
    count, done, sent, waited = {}, {}, 0, set()
    for i, o in enumerate(ops):
        if o["kind"] == "ext":
            continue
        q = o["q"]
        for kind, v in waits[i]:
            if kind == "q":
                queues[q].wait_ge(T.sem["q_%s%d" % (q, v[0])], v[1])
                done[(q, v[0])] = v[1]
            else:
                queues[q].wait_ge(T.sem[names[v]], total[v])
                waited.add(v)
        x = o["fn"]()
        if o["kind"] == "remote":
            sent += o["n"]
        elif i in names:
            x.then_inc(T.sem[names[i]], o["n"])
        else:
            r = sum(count.get((q, n), 0) for n in range(KQ[q])) % KQ[q]
            x.then_inc(T.sem["q_%s%d" % (q, r)], 1)
            count[(q, r)] = count.get((q, r), 0) + 1
    for q, r in count:
        if done.get((q, r), 0) < count[(q, r)]:
            queues[q].wait_ge(T.sem["q_%s%d" % (q, r)], count[(q, r)])
    g.wait_ge(T.sem["sent"], sent)
    for i in total:
        if i not in waited:
            queues[ops[i]["q"]].wait_ge(T.sem[names[i]], total[i])
